import numpy as np
import ml_dtypes


def mxq(x, axis, fmt="e4m3"):
    dtype, down = {"e4m3": (ml_dtypes.float8_e4m3fn, 7), "e5m2": (ml_dtypes.float8_e5m2, 14)}[fmt]
    v = np.moveaxis(np.asarray(x, np.float32).astype(ml_dtypes.bfloat16).astype(np.float64), axis, -1)
    blocks = v.reshape(v.shape[:-1] + (-1, 32))
    amax = np.abs(blocks).max(-1, keepdims=True)
    byte = np.maximum(np.where(amax > 0, np.frexp(amax)[1] - 1 + 127, 0) - down, 1)
    scale = np.exp2(byte - 127.0)
    codes = (blocks / scale).astype(np.float32).astype(dtype).astype(np.float64)
    return np.moveaxis((codes * scale).reshape(v.shape), -1, axis)


WIDE = False


def mx_kscale(k):
    if not WIDE:
        return np.ones(k)
    levels = np.array([10, -10, 5, -5, 0])
    if k % 512:
        return np.exp2(np.random.permutation(np.resize(levels, k // 32))).repeat(32)
    a = np.empty((k // 512, 16))
    for p in range(k // 512):
        a[p, :8] = np.random.permutation(np.resize(levels, 8))
        for g in range(8):
            far = levels[np.abs(levels - a[p, g]) >= 10]
            a[p, g + 8] = far[np.random.randint(len(far))]
    return np.exp2(a.ravel()).repeat(32)


def f64(x):
    return np.asarray(x).astype(np.float64)


def striped(idx):
    return np.tile(idx.reshape(-1, 16).T, (8, 1)).astype(np.uint16)


def unstriped(offs):
    return offs[:16].T.reshape(-1).astype(np.int64)


def pack_weight(w):
    k, n = w.shape
    w = f64(np.asarray(w, np.float32).astype(ml_dtypes.bfloat16)).reshape(k // 32, 32, n)
    amax = np.abs(w).max(1)
    byte = np.clip(np.where(amax > 0, np.frexp(amax)[1] - 1 + 127 - 7, 1), 1, 254)
    scaled = (w * np.exp2(127.0 - byte)[:, None, :]).reshape(k, n).astype(np.float32)
    words = np.ascontiguousarray(scaled.reshape(k // 512, 128, 4, n).transpose(0, 1, 3, 2)).astype(ml_dtypes.float8_e4m3fn).view(np.uint8)
    return words, np.ascontiguousarray(byte.astype(np.uint8).reshape(k // 512, 16, n))


def unpack_weight(words, scales):
    g, p, n, _ = words.shape
    vals = np.ascontiguousarray(words).view(ml_dtypes.float8_e4m3fn).astype(np.float64) * np.repeat(np.exp2(scales.astype(np.float64) - 127.0), 8, axis=1)[..., None]
    return vals.transpose(0, 1, 3, 2).reshape(g * 512, n)


def silu(v):
    return v / (1.0 + np.exp(-np.maximum(v, -700.0)))


K, T, S, N, R = 1024, 2048, 512, 128, 256


def setup_inputs():
    n = np.random.standard_normal
    s = mx_kscale(K)[:, None]
    packed_xT = pack_weight(n((K, T)) * s)
    return {
        "x_words": packed_xT[0],
        "x_scales": packed_xT[1],
        "w1": (n((K, N)) / np.sqrt(K) / s).astype(np.float32),
        "gam": (np.random.uniform(0.5, 1.5, (N, R))).astype(np.float32),
        "bet": (0.5 * n((N, R))).astype(np.float32),
        "offs": striped(np.random.permutation(T)[:S]),
        "lab": striped(np.random.permutation(np.concatenate([np.arange(R), np.random.randint(0, R, S - R)]))),
    }


def reference(x_words, x_scales, w1, gam, bet, offs, lab):
    xq = unpack_weight(x_words, x_scales)[:, unstriped(offs)]
    y = mxq(f64(w1), 0, "e4m3").T @ xq
    my = y.mean(axis=1, keepdims=True)
    dy = y - my
    qy = (dy) ** 2
    sy = np.sqrt(qy.mean(axis=1, keepdims=True) + 1e-4)
    return silu((dy / sy) * f64(gam)[:, unstriped(lab)] + f64(bet)[:, unstriped(lab)])

@@ -1,0 +1,117 @@
+from contextlib import ExitStack
+
+import concourse.mybir as mybir
+
+K, T, S, N, R = 1024, 2048, 512, 128, 256
+FLOPS = 2 * K * N * S
+EPS = 1e-4
+
+F32 = mybir.dt.float32
+BF16 = mybir.dt.bfloat16
+I32 = mybir.dt.int32
+U32 = mybir.dt.uint32
+U16 = mybir.dt.uint16
+U8 = mybir.dt.uint8
+FP8X4 = mybir.dt.float8_e4m3fn_x4
+ALU = mybir.AluOpType
+ACT = mybir.ActivationFunctionType
+
+P = 128
+PACK = 4
+PASSES = K // (P * PACK)
+HALF = S // 2
+WINDOW = 3 * R
+
+
+def tile_picked_yspade_silu_p_kernel(tc, x_words, x_scales, w1, gam, bet, offs, lab, out):
+    nc = tc.nc
+    with ExitStack() as ctx:
+        keep = ctx.enter_context(tc.tile_pool(name="keep", bufs=1))
+        psum = ctx.enter_context(tc.psum_pool(name="psum", bufs=1))
+
+        offs_sb = keep.tile([P, S // 16], U16, name="offs_sb")
+        lab_sb = keep.tile([P, S // 16], U16, name="lab_sb")
+        gam_sb = keep.tile([P, WINDOW], F32, name="gam_sb")
+        bet_sb = keep.tile([P, WINDOW], F32, name="bet_sb")
+        scale_sb = keep.tile([P, T], U8, name="scale_sb", align_bytes=64)
+        word_sb = [keep.tile([P, T], U32, name="word_sb%d" % o, align_bytes=64) for o in range(PASSES)]
+        w_raw = keep.tile([P, PASSES, PACK, N], F32, name="w_raw")
+        minus_half = keep.tile([P, 1], F32, name="minus_half")
+
+        nc.vector.memset(scale_sb[:].bitcast(I32), 0)
+        nc.gpsimd.memset(gam_sb[:, R:], 0.0)
+        nc.gpsimd.memset(bet_sb[:, R:], 0.0)
+        nc.gpsimd.memset(minus_half[:], -0.5)
+
+        nc.sync.dma_start(lab_sb[:], lab)
+        nc.sync.dma_start(gam_sb[:, :R], gam)
+        nc.sync.dma_start(bet_sb[:, :R], bet)
+        nc.sync.dma_start(offs_sb[:], offs)
+        for q in range(4):
+            nc.scalar.dma_start(
+                scale_sb[32 * q : 32 * q + 4 * PASSES, :].bitcast(I32),
+                x_scales[:, 4 * q : 4 * q + 4, :].bitcast(I32),
+            )
+        nc.sync.dma_start(w_raw[:], w1.rearrange("(o p j) m -> p o j m", o=PASSES, j=PACK))
+        for o in range(PASSES):
+            nc.sync.dma_start(word_sb[o][:].bitcast(I32), x_words[o].rearrange("p c j -> p (c j)").bitcast(I32))
+
+        gam_px = keep.tile([P, S], F32, name="gam_px")
+        bet_px = keep.tile([P, S], F32, name="bet_px")
+        nc.vector.tensor_copy(gam_px[:], gam_sb[:].indirect(lab_sb[:]))
+        nc.vector.tensor_copy(bet_px[:], bet_sb[:].indirect(lab_sb[:]))
+
+        w_grouped = keep.tile([P, PASSES, N, PACK], BF16, name="w_grouped", align_bytes=64)
+        nc.scalar.copy(w_grouped[:], w_raw[:].rearrange("p o j m -> p o m j"))
+        w_codes = keep.tile([P, PASSES * N], U32, name="w_codes", align_bytes=64)
+        w_scales = keep.tile([P, PASSES * N], U8, name="w_scales", align_bytes=64)
+
+        scale_px = keep.tile([P, S], U8, name="scale_px", align_bytes=64)
+        nc.vector.tensor_copy(scale_px[:], scale_sb[:].indirect(offs_sb[:]))
+        nc.vector.quantize_mx(
+            out=w_codes[:].bitcast(FP8X4), scales=w_scales[:], in_=w_grouped[:].rearrange("p o m j -> p (o m j)")
+        )
+
+        word_px = [keep.tile([P, S], U32, name="word_px%d" % o, align_bytes=64) for o in range(PASSES)]
+        nc.vector.tensor_copy(word_px[0][:], word_sb[0][:].indirect(offs_sb[:]))
+        halves = [slice(h * HALF, (h + 1) * HALF) for h in range(2)]
+        for h in range(2):
+            nc.vector.tensor_copy(
+                word_px[1][:, halves[h]], word_sb[1][:].indirect(offs_sb[:, h * HALF // 16 : (h + 1) * HALF // 16])
+            )
+
+        y = [psum.tile([P, HALF], F32, name="y%d" % h) for h in range(2)]
+        for o in range(PASSES):
+            for h in range(2):
+                nc.tensor.matmul_mx(
+                    out=y[h][:],
+                    lhsT=w_codes[:, o * N : (o + 1) * N].bitcast(FP8X4),
+                    lhsT_scale=w_scales[:, o * N : (o + 1) * N],
+                    rhs=word_px[o][:, halves[h]].bitcast(FP8X4),
+                    rhs_scale=scale_px[4 * o : P, halves[h]],
+                    start=(o == 0),
+                    stop=(o == PASSES - 1),
+                )
+
+        stats = keep.tile([P, 12], F32, name="stats")
+        mean_var = keep.tile([P, 2], F32, name="mean_var")
+        rstd = keep.tile([P, 1], F32, name="rstd")
+        nc.vector.bn_stats(stats[:, 0:6], y[0][:])
+        nc.vector.tensor_scalar_add(stats[:, 2:3], stats[:, 2:3], S * EPS)
+        nc.vector.bn_stats(stats[:, 6:12], y[1][:])
+        nc.vector.bn_aggr(mean_var[:], stats[:])
+        nc.gpsimd.tensor_tensor(rstd[:], mean_var[:, 1:2], minus_half[:], ALU.pow)
+
+        scaled = keep.tile([P, S], F32, name="scaled")
+        shifted = keep.tile([P, S], F32, name="shifted")
+        result = keep.tile([P, S], F32, name="result")
+        for h in range(2):
+            nc.vector.scalar_tensor_tensor(
+                scaled[:, halves[h]], y[h][:], mean_var[:, 0:1], gam_px[:, halves[h]], ALU.subtract, ALU.mult
+            )
+        for h in range(2):
+            nc.vector.scalar_tensor_tensor(
+                shifted[:, halves[h]], scaled[:, halves[h]], rstd[:], bet_px[:, halves[h]], ALU.mult, ALU.add
+            )
+            nc.scalar.activation(result[:, halves[h]], shifted[:, halves[h]], ACT.Silu)
+            nc.sync.dma_start(out[:, halves[h]], result[:, halves[h]])

@@ -38,27 +38,39 @@ def tile_picked_yspade_silu_p_kernel(tc, x_words, x_scales, w1, gam, bet, offs, 
         w_raw = keep.tile([P, PASSES, PACK, N], F32, name="w_raw")
         minus_half = keep.tile([P, 1], F32, name="minus_half")
 
+        warm = keep.tile([P, 2], F32, name="warm")
         nc.vector.memset(scale_sb[:].bitcast(I32), 0)
-        nc.gpsimd.memset(gam_sb[:, R:], 0.0)
-        nc.gpsimd.memset(bet_sb[:, R:], 0.0)
         nc.gpsimd.memset(minus_half[:], -0.5)
+        nc.gpsimd.memset(warm[:, 0:1], 1.0)
+        nc.gpsimd.tensor_tensor(warm[:, 1:2], warm[:, 0:1], minus_half[:], ALU.pow)
+        warm_act = keep.tile([P, 1], F32, name="warm_act")
+        nc.scalar.activation(warm_act[:], minus_half[:], ACT.Silu)
+        nc.vector.memset(gam_sb[:, R:], 0.0)
+        nc.vector.memset(bet_sb[:, R:], 0.0)
 
-        nc.sync.dma_start(lab_sb[:], lab)
         nc.sync.dma_start(gam_sb[:, :R], gam)
-        nc.sync.dma_start(bet_sb[:, :R], bet)
         nc.sync.dma_start(offs_sb[:], offs)
-        for q in range(4):
-            nc.scalar.dma_start(
-                scale_sb[32 * q : 32 * q + 4 * PASSES, :].bitcast(I32),
-                x_scales[:, 4 * q : 4 * q + 4, :].bitcast(I32),
-            )
+        for o in range(PASSES):
+            nc.sync.dma_start(scale_sb[4 * o : P : 8, :].bitcast(I32), x_scales[o].bitcast(I32))
+        nc.sync.dma_start(bet_sb[:, :R], bet)
+        nc.sync.dma_start(lab_sb[:], lab)
         nc.sync.dma_start(w_raw[:], w1.rearrange("(o p j) m -> p o j m", o=PASSES, j=PACK))
         for o in range(PASSES):
             nc.sync.dma_start(word_sb[o][:].bitcast(I32), x_words[o].rearrange("p c j -> p (c j)").bitcast(I32))
 
+        scale_spread = keep.tile([P, S], U8, name="scale_spread", align_bytes=64)
+        scale_px = keep.tile([P, S], U8, name="scale_px", align_bytes=64)
+        nc.vector.tensor_copy(scale_spread[:], scale_sb[:].indirect(offs_sb[:]))
+        nc.vector.tensor_copy(scale_px[:].bitcast(I32), scale_spread[:].bitcast(I32))
+        for o in range(PASSES):
+            for r in range(1, 4):
+                nc.scalar.dma_start(
+                    scale_px[4 * o + r : P : 32, :].bitcast(I32), scale_spread[4 * o + 8 * r : P : 32, :].bitcast(I32)
+                )
+
         gam_px = keep.tile([P, S], F32, name="gam_px")
-        bet_px = keep.tile([P, S], F32, name="bet_px")
         nc.vector.tensor_copy(gam_px[:], gam_sb[:].indirect(lab_sb[:]))
+        bet_px = keep.tile([P, S], F32, name="bet_px")
         nc.vector.tensor_copy(bet_px[:], bet_sb[:].indirect(lab_sb[:]))
 
         w_grouped = keep.tile([P, PASSES, N, PACK], BF16, name="w_grouped", align_bytes=64)
@@ -66,8 +78,6 @@ def tile_picked_yspade_silu_p_kernel(tc, x_words, x_scales, w1, gam, bet, offs, 
         w_codes = keep.tile([P, PASSES * N], U32, name="w_codes", align_bytes=64)
         w_scales = keep.tile([P, PASSES * N], U8, name="w_scales", align_bytes=64)
 
-        scale_px = keep.tile([P, S], U8, name="scale_px", align_bytes=64)
-        nc.vector.tensor_copy(scale_px[:], scale_sb[:].indirect(offs_sb[:]))
         nc.vector.quantize_mx(
             out=w_codes[:].bitcast(FP8X4), scales=w_scales[:], in_=w_grouped[:].rearrange("p o m j -> p (o m j)")
         )
@@ -109,9 +119,9 @@ def tile_picked_yspade_silu_p_kernel(tc, x_words, x_scales, w1, gam, bet, offs, 
             nc.vector.scalar_tensor_tensor(
                 scaled[:, halves[h]], y[h][:], mean_var[:, 0:1], gam_px[:, halves[h]], ALU.subtract, ALU.mult
             )
-        for h in range(2):
+        for cols in (slice(0, 256), slice(256, 384), slice(384, 512)):
             nc.vector.scalar_tensor_tensor(
-                shifted[:, halves[h]], scaled[:, halves[h]], rstd[:], bet_px[:, halves[h]], ALU.mult, ALU.add
+                shifted[:, cols], scaled[:, cols], rstd[:], bet_px[:, cols], ALU.mult, ALU.add
             )
-            nc.scalar.activation(result[:, halves[h]], shifted[:, halves[h]], ACT.Silu)
-            nc.sync.dma_start(out[:, halves[h]], result[:, halves[h]])
+            nc.scalar.activation(result[:, cols], shifted[:, cols], ACT.Silu)
+            nc.sync.dma_start(out[:, cols], result[:, cols])

@@ -49,10 +49,10 @@ def tile_picked_yspade_silu_p_kernel(tc, x_words, x_scales, w1, gam, bet, offs, 
         nc.vector.memset(bet_sb[:, R:], 0.0)
 
         nc.sync.dma_start(gam_sb[:, :R], gam)
+        nc.sync.dma_start(bet_sb[:, :R], bet)
         nc.sync.dma_start(offs_sb[:], offs)
         for o in range(PASSES):
             nc.sync.dma_start(scale_sb[4 * o : P : 8, :].bitcast(I32), x_scales[o].bitcast(I32))
-        nc.sync.dma_start(bet_sb[:, :R], bet)
         nc.sync.dma_start(lab_sb[:], lab)
         nc.sync.dma_start(w_raw[:], w1.rearrange("(o p j) m -> p o j m", o=PASSES, j=PACK))
         for o in range(PASSES):
@@ -119,7 +119,7 @@ def tile_picked_yspade_silu_p_kernel(tc, x_words, x_scales, w1, gam, bet, offs, 
             nc.vector.scalar_tensor_tensor(
                 scaled[:, halves[h]], y[h][:], mean_var[:, 0:1], gam_px[:, halves[h]], ALU.subtract, ALU.mult
             )
-        for cols in (slice(0, 256), slice(256, 384), slice(384, 512)):
+        for cols in [slice(c, c + 128) for c in range(0, S, 128)]:
             nc.vector.scalar_tensor_tensor(
                 shifted[:, cols], scaled[:, cols], rstd[:], bet_px[:, cols], ALU.mult, ALU.add
             )

@@ -90,38 +90,41 @@ def tile_picked_yspade_silu_p_kernel(tc, x_words, x_scales, w1, gam, bet, offs, 
                 word_px[1][:, halves[h]], word_sb[1][:].indirect(offs_sb[:, h * HALF // 16 : (h + 1) * HALF // 16])
             )
 
-        y = [psum.tile([P, HALF], F32, name="y%d" % h) for h in range(2)]
+        pieces = [slice(0, HALF), slice(HALF, HALF + 128), slice(HALF + 128, S)]
+        y = [psum.tile([P, c.stop - c.start], F32, name="y%d" % h) for h, c in enumerate(pieces)]
         for o in range(PASSES):
-            for h in range(2):
+            for h, c in enumerate(pieces):
                 nc.tensor.matmul_mx(
                     out=y[h][:],
                     lhsT=w_codes[:, o * N : (o + 1) * N].bitcast(FP8X4),
                     lhsT_scale=w_scales[:, o * N : (o + 1) * N],
-                    rhs=word_px[o][:, halves[h]].bitcast(FP8X4),
-                    rhs_scale=scale_px[4 * o : P, halves[h]],
+                    rhs=word_px[o][:, c].bitcast(FP8X4),
+                    rhs_scale=scale_px[4 * o : P, c],
                     start=(o == 0),
                     stop=(o == PASSES - 1),
                 )
 
-        stats = keep.tile([P, 12], F32, name="stats")
+        stats = keep.tile([P, 18], F32, name="stats")
         mean_var = keep.tile([P, 2], F32, name="mean_var")
         rstd = keep.tile([P, 1], F32, name="rstd")
         nc.vector.bn_stats(stats[:, 0:6], y[0][:])
         nc.vector.tensor_scalar_add(stats[:, 2:3], stats[:, 2:3], S * EPS)
         nc.vector.bn_stats(stats[:, 6:12], y[1][:])
+        nc.vector.bn_stats(stats[:, 12:18], y[2][:])
         nc.vector.bn_aggr(mean_var[:], stats[:])
         nc.gpsimd.tensor_tensor(rstd[:], mean_var[:, 1:2], minus_half[:], ALU.pow)
 
         scaled = keep.tile([P, S], F32, name="scaled")
         shifted = keep.tile([P, S], F32, name="shifted")
         result = keep.tile([P, S], F32, name="result")
-        for h in range(2):
+        for h, c in enumerate(pieces):
             nc.vector.scalar_tensor_tensor(
-                scaled[:, halves[h]], y[h][:], mean_var[:, 0:1], gam_px[:, halves[h]], ALU.subtract, ALU.mult
+                scaled[:, c], y[h][:], mean_var[:, 0:1], gam_px[:, c], ALU.subtract, ALU.mult
             )
         for cols in [slice(c, c + 128) for c in range(0, S, 128)]:
             nc.vector.scalar_tensor_tensor(
                 shifted[:, cols], scaled[:, cols], rstd[:], bet_px[:, cols], ALU.mult, ALU.add
             )
             nc.scalar.activation(result[:, cols], shifted[:, cols], ACT.Silu)
-            nc.sync.dma_start(out[:, cols], result[:, cols])
+            queue = nc.scalar if cols.stop == S else nc.sync
+            queue.dma_start(out[:, cols], result[:, cols])

@@ -19,7 +19,9 @@ ACT = mybir.ActivationFunctionType
 P = 128
 PACK = 4
 PASSES = K // (P * PACK)
+LIST_ROWS = 16
 HALF = S // 2
+QUARTER = S // 4
 WINDOW = 3 * R
 
 
@@ -29,8 +31,8 @@ def tile_picked_yspade_silu_p_kernel(tc, x_words, x_scales, w1, gam, bet, offs, 
         keep = ctx.enter_context(tc.tile_pool(name="keep", bufs=1))
         psum = ctx.enter_context(tc.psum_pool(name="psum", bufs=1))
 
-        offs_sb = keep.tile([P, S // 16], U16, name="offs_sb")
-        lab_sb = keep.tile([P, S // 16], U16, name="lab_sb")
+        offs_sb = keep.tile([P, S // LIST_ROWS], U16, name="offs_sb")
+        lab_sb = keep.tile([P, S // LIST_ROWS], U16, name="lab_sb")
         gam_sb = keep.tile([P, WINDOW], F32, name="gam_sb")
         bet_sb = keep.tile([P, WINDOW], F32, name="bet_sb")
         scale_sb = keep.tile([P, T], U8, name="scale_sb", align_bytes=64)
@@ -38,11 +40,8 @@ def tile_picked_yspade_silu_p_kernel(tc, x_words, x_scales, w1, gam, bet, offs, 
         w_raw = keep.tile([P, PASSES, PACK, N], F32, name="w_raw")
         minus_half = keep.tile([P, 1], F32, name="minus_half")
 
-        warm = keep.tile([P, 2], F32, name="warm")
         nc.vector.memset(scale_sb[:].bitcast(I32), 0)
         nc.gpsimd.memset(minus_half[:], -0.5)
-        nc.gpsimd.memset(warm[:, 0:1], 1.0)
-        nc.gpsimd.tensor_tensor(warm[:, 1:2], warm[:, 0:1], minus_half[:], ALU.pow)
         warm_act = keep.tile([P, 1], F32, name="warm_act")
         nc.scalar.activation(warm_act[:], minus_half[:], ACT.Silu)
         nc.vector.memset(gam_sb[:, R:], 0.0)
@@ -53,8 +52,8 @@ def tile_picked_yspade_silu_p_kernel(tc, x_words, x_scales, w1, gam, bet, offs, 
         nc.sync.dma_start(offs_sb[:], offs)
         for o in range(PASSES):
             nc.sync.dma_start(scale_sb[4 * o : P : 8, :].bitcast(I32), x_scales[o].bitcast(I32))
-        nc.sync.dma_start(lab_sb[:], lab)
         nc.sync.dma_start(w_raw[:], w1.rearrange("(o p j) m -> p o j m", o=PASSES, j=PACK))
+        nc.sync.dma_start(lab_sb[:], lab)
         for o in range(PASSES):
             nc.sync.dma_start(word_sb[o][:].bitcast(I32), x_words[o].rearrange("p c j -> p (c j)").bitcast(I32))
 
@@ -77,51 +76,49 @@ def tile_picked_yspade_silu_p_kernel(tc, x_words, x_scales, w1, gam, bet, offs, 
         nc.scalar.copy(w_grouped[:], w_raw[:].rearrange("p o j m -> p o m j"))
         w_codes = keep.tile([P, PASSES * N], U32, name="w_codes", align_bytes=64)
         w_scales = keep.tile([P, PASSES * N], U8, name="w_scales", align_bytes=64)
-
         nc.vector.quantize_mx(
             out=w_codes[:].bitcast(FP8X4), scales=w_scales[:], in_=w_grouped[:].rearrange("p o m j -> p (o m j)")
         )
 
         word_px = [keep.tile([P, S], U32, name="word_px%d" % o, align_bytes=64) for o in range(PASSES)]
         nc.vector.tensor_copy(word_px[0][:], word_sb[0][:].indirect(offs_sb[:]))
-        halves = [slice(h * HALF, (h + 1) * HALF) for h in range(2)]
-        for h in range(2):
-            nc.vector.tensor_copy(
-                word_px[1][:, halves[h]], word_sb[1][:].indirect(offs_sb[:, h * HALF // 16 : (h + 1) * HALF // 16])
-            )
+        for first in range(0, S, HALF):
+            entries = offs_sb[:, first // LIST_ROWS : (first + HALF) // LIST_ROWS]
+            nc.vector.tensor_copy(word_px[1][:, first : first + HALF], word_sb[1][:].indirect(entries))
 
-        pieces = [slice(0, HALF), slice(HALF, HALF + 128), slice(HALF + 128, S)]
-        y = [psum.tile([P, c.stop - c.start], F32, name="y%d" % h) for h, c in enumerate(pieces)]
+        banks = [slice(0, HALF), slice(HALF, HALF + QUARTER), slice(HALF + QUARTER, S)]
+        y = [psum.tile([P, cols.stop - cols.start], F32, name="y%d" % b) for b, cols in enumerate(banks)]
         for o in range(PASSES):
-            for h, c in enumerate(pieces):
+            for b, cols in enumerate(banks):
                 nc.tensor.matmul_mx(
-                    out=y[h][:],
+                    out=y[b][:],
                     lhsT=w_codes[:, o * N : (o + 1) * N].bitcast(FP8X4),
                     lhsT_scale=w_scales[:, o * N : (o + 1) * N],
-                    rhs=word_px[o][:, c].bitcast(FP8X4),
-                    rhs_scale=scale_px[4 * o : P, c],
+                    rhs=word_px[o][:, cols].bitcast(FP8X4),
+                    rhs_scale=scale_px[4 * o : P, cols],
                     start=(o == 0),
                     stop=(o == PASSES - 1),
                 )
 
-        stats = keep.tile([P, 18], F32, name="stats")
+        stats = keep.tile([P, 6 * len(banks)], F32, name="stats")
         mean_var = keep.tile([P, 2], F32, name="mean_var")
         rstd = keep.tile([P, 1], F32, name="rstd")
         nc.vector.bn_stats(stats[:, 0:6], y[0][:])
         nc.vector.tensor_scalar_add(stats[:, 2:3], stats[:, 2:3], S * EPS)
-        nc.vector.bn_stats(stats[:, 6:12], y[1][:])
-        nc.vector.bn_stats(stats[:, 12:18], y[2][:])
+        for b in range(1, len(banks)):
+            nc.vector.bn_stats(stats[:, 6 * b : 6 * b + 6], y[b][:])
         nc.vector.bn_aggr(mean_var[:], stats[:])
         nc.gpsimd.tensor_tensor(rstd[:], mean_var[:, 1:2], minus_half[:], ALU.pow)
 
         scaled = keep.tile([P, S], F32, name="scaled")
         shifted = keep.tile([P, S], F32, name="shifted")
         result = keep.tile([P, S], F32, name="result")
-        for h, c in enumerate(pieces):
+        for b, cols in enumerate(banks):
             nc.vector.scalar_tensor_tensor(
-                scaled[:, c], y[h][:], mean_var[:, 0:1], gam_px[:, c], ALU.subtract, ALU.mult
+                scaled[:, cols], y[b][:], mean_var[:, 0:1], gam_px[:, cols], ALU.subtract, ALU.mult
             )
-        for cols in [slice(c, c + 128) for c in range(0, S, 128)]:
+        for first in range(0, S, QUARTER):
+            cols = slice(first, first + QUARTER)
             nc.vector.scalar_tensor_tensor(
                 shifted[:, cols], scaled[:, cols], rstd[:], bet_px[:, cols], ALU.mult, ALU.add
             )

@@ -44,28 +44,26 @@ def tile_picked_yspade_silu_p_kernel(tc, x_words, x_scales, w1, gam, bet, offs, 
         nc.gpsimd.memset(minus_half[:], -0.5)
         warm_act = keep.tile([P, 1], F32, name="warm_act")
         nc.scalar.activation(warm_act[:], minus_half[:], ACT.Silu)
+        scale_px = keep.tile([P, PASSES * S], U8, name="scale_px", align_bytes=64)
+        nc.vector.memset(scale_px[:].bitcast(I32), 0)
         nc.vector.memset(gam_sb[:, R:], 0.0)
         nc.vector.memset(bet_sb[:, R:], 0.0)
 
         nc.sync.dma_start(gam_sb[:, :R], gam)
         nc.sync.dma_start(bet_sb[:, :R], bet)
         nc.sync.dma_start(offs_sb[:], offs)
-        for o in range(PASSES):
-            nc.sync.dma_start(scale_sb[4 * o : P : 8, :].bitcast(I32), x_scales[o].bitcast(I32))
+        nc.sync.dma_start(scale_sb[0:P:4, :].bitcast(I32), x_scales.bitcast(I32).rearrange("o i c -> i o c"))
         nc.sync.dma_start(w_raw[:], w1.rearrange("(o p j) m -> p o j m", o=PASSES, j=PACK))
         nc.sync.dma_start(lab_sb[:], lab)
         for o in range(PASSES):
             nc.sync.dma_start(word_sb[o][:].bitcast(I32), x_words[o].rearrange("p c j -> p (c j)").bitcast(I32))
 
         scale_spread = keep.tile([P, S], U8, name="scale_spread", align_bytes=64)
-        scale_px = keep.tile([P, S], U8, name="scale_px", align_bytes=64)
         nc.vector.tensor_copy(scale_spread[:], scale_sb[:].indirect(offs_sb[:]))
-        nc.vector.tensor_copy(scale_px[:].bitcast(I32), scale_spread[:].bitcast(I32))
-        for o in range(PASSES):
-            for r in range(1, 4):
-                nc.scalar.dma_start(
-                    scale_px[4 * o + r : P : 32, :].bitcast(I32), scale_spread[4 * o + 8 * r : P : 32, :].bitcast(I32)
-                )
+        for q in range(4):
+            nc.scalar.dma_start(
+                scale_px[32 * q : 32 * q + 4, :].bitcast(I32), scale_spread[32 * q : 32 * q + 32 : 4, :].bitcast(I32)
+            )
 
         gam_px = keep.tile([P, S], F32, name="gam_px")
         nc.vector.tensor_copy(gam_px[:], gam_sb[:].indirect(lab_sb[:]))
@@ -95,7 +93,7 @@ def tile_picked_yspade_silu_p_kernel(tc, x_words, x_scales, w1, gam, bet, offs, 
                     lhsT=w_codes[:, o * N : (o + 1) * N].bitcast(FP8X4),
                     lhsT_scale=w_scales[:, o * N : (o + 1) * N],
                     rhs=word_px[o][:, cols].bitcast(FP8X4),
-                    rhs_scale=scale_px[4 * o : P, cols],
+                    rhs_scale=scale_px[:, o * S + cols.start : o * S + cols.stop],
                     start=(o == 0),
                     stop=(o == PASSES - 1),
                 )

@@ -22,7 +22,7 @@ PASSES = K // (P * PACK)
 LIST_ROWS = 16
 HALF = S // 2
 QUARTER = S // 4
-WINDOW = 3 * R
+WINDOW = R + 8
 
 
 def tile_picked_yspade_silu_p_kernel(tc, x_words, x_scales, w1, gam, bet, offs, lab, out):
@@ -35,7 +35,7 @@ def tile_picked_yspade_silu_p_kernel(tc, x_words, x_scales, w1, gam, bet, offs, 
         lab_sb = keep.tile([P, S // LIST_ROWS], U16, name="lab_sb")
         gam_sb = keep.tile([P, WINDOW], F32, name="gam_sb")
         bet_sb = keep.tile([P, WINDOW], F32, name="bet_sb")
-        scale_sb = keep.tile([P, T], U8, name="scale_sb", align_bytes=64)
+        scale_sb = keep.tile([P, T], U8, name="scale_sb", tag="shared", align_bytes=64)
         word_sb = [keep.tile([P, T], U32, name="word_sb%d" % o, align_bytes=64) for o in range(PASSES)]
         w_raw = keep.tile([P, PASSES, PACK, N], F32, name="w_raw")
         minus_half = keep.tile([P, 1], F32, name="minus_half")
@@ -51,24 +51,26 @@ def tile_picked_yspade_silu_p_kernel(tc, x_words, x_scales, w1, gam, bet, offs, 
 
         nc.sync.dma_start(gam_sb[:, :R], gam)
         nc.sync.dma_start(bet_sb[:, :R], bet)
+        nc.sync.dma_start(lab_sb[:], lab)
         nc.sync.dma_start(offs_sb[:], offs)
         nc.sync.dma_start(scale_sb[0:P:4, :].bitcast(I32), x_scales.bitcast(I32).rearrange("o i c -> i o c"))
         nc.sync.dma_start(w_raw[:], w1.rearrange("(o p j) m -> p o j m", o=PASSES, j=PACK))
-        nc.sync.dma_start(lab_sb[:], lab)
         for o in range(PASSES):
             nc.sync.dma_start(word_sb[o][:].bitcast(I32), x_words[o].rearrange("p c j -> p (c j)").bitcast(I32))
 
         scale_spread = keep.tile([P, S], U8, name="scale_spread", align_bytes=64)
         nc.vector.tensor_copy(scale_spread[:], scale_sb[:].indirect(offs_sb[:]))
         for q in range(4):
-            nc.scalar.dma_start(
+            nc.sync.dma_start(
                 scale_px[32 * q : 32 * q + 4, :].bitcast(I32), scale_spread[32 * q : 32 * q + 32 : 4, :].bitcast(I32)
             )
 
         gam_px = keep.tile([P, S], F32, name="gam_px")
-        nc.vector.tensor_copy(gam_px[:], gam_sb[:].indirect(lab_sb[:]))
-        bet_px = keep.tile([P, S], F32, name="bet_px")
-        nc.vector.tensor_copy(bet_px[:], bet_sb[:].indirect(lab_sb[:]))
+        bet_px = keep.tile([P, S], F32, name="bet_px", tag="shared", align_bytes=64)
+        for table, picked in ((gam_sb, gam_px), (bet_sb, bet_px)):
+            for first in range(0, S, HALF):
+                entries = lab_sb[:, first // LIST_ROWS : (first + HALF) // LIST_ROWS]
+                nc.vector.tensor_copy(picked[:, first : first + HALF], table[:].indirect(entries))
 
         w_grouped = keep.tile([P, PASSES, N, PACK], BF16, name="w_grouped", align_bytes=64)
         nc.scalar.copy(w_grouped[:], w_raw[:].rearrange("p o j m -> p o m j"))
@@ -121,5 +123,4 @@ def tile_picked_yspade_silu_p_kernel(tc, x_words, x_scales, w1, gam, bet, offs, 
                 shifted[:, cols], scaled[:, cols], rstd[:], bet_px[:, cols], ALU.mult, ALU.add
             )
             nc.scalar.activation(result[:, cols], shifted[:, cols], ACT.Silu)
-            queue = nc.scalar if cols.stop == S else nc.sync
-            queue.dma_start(out[:, cols], result[:, cols])
+            nc.sync.dma_start(out[:, cols], result[:, cols])

@@ -19,7 +19,11 @@ ACT = mybir.ActivationFunctionType
 P = 128
 PACK = 4
 PASSES = K // (P * PACK)
+STATS = 6
 LIST_ROWS = 16
+QUADRANT = 32
+SCALE_ROWS = 4
+SPREAD = QUADRANT // (PASSES * SCALE_ROWS)
 HALF = S // 2
 QUARTER = S // 4
 WINDOW = R + 8
@@ -35,38 +39,37 @@ def tile_picked_yspade_silu_p_kernel(tc, x_words, x_scales, w1, gam, bet, offs, 
         lab_sb = keep.tile([P, S // LIST_ROWS], U16, name="lab_sb")
         gam_sb = keep.tile([P, WINDOW], F32, name="gam_sb")
         bet_sb = keep.tile([P, WINDOW], F32, name="bet_sb")
-        scale_sb = keep.tile([P, T], U8, name="scale_sb", tag="shared", align_bytes=64)
+        scale_sb = keep.tile([P, T], U8, name="scale_sb", align_bytes=64)
         word_sb = [keep.tile([P, T], U32, name="word_sb%d" % o, align_bytes=64) for o in range(PASSES)]
         w_raw = keep.tile([P, PASSES, PACK, N], F32, name="w_raw")
         minus_half = keep.tile([P, 1], F32, name="minus_half")
 
         nc.vector.memset(scale_sb[:].bitcast(I32), 0)
-        nc.gpsimd.memset(minus_half[:], -0.5)
-        warm_act = keep.tile([P, 1], F32, name="warm_act")
-        nc.scalar.activation(warm_act[:], minus_half[:], ACT.Silu)
         scale_px = keep.tile([P, PASSES * S], U8, name="scale_px", align_bytes=64)
         nc.vector.memset(scale_px[:].bitcast(I32), 0)
         nc.vector.memset(gam_sb[:, R:], 0.0)
         nc.vector.memset(bet_sb[:, R:], 0.0)
+        nc.vector.memset(minus_half[:], -0.5)
 
         nc.sync.dma_start(gam_sb[:, :R], gam)
-        nc.sync.dma_start(bet_sb[:, :R], bet)
         nc.sync.dma_start(lab_sb[:], lab)
         nc.sync.dma_start(offs_sb[:], offs)
-        nc.sync.dma_start(scale_sb[0:P:4, :].bitcast(I32), x_scales.bitcast(I32).rearrange("o i c -> i o c"))
         nc.sync.dma_start(w_raw[:], w1.rearrange("(o p j) m -> p o j m", o=PASSES, j=PACK))
+        nc.sync.dma_start(scale_sb[0:P:SPREAD, :].bitcast(I32), x_scales.bitcast(I32).rearrange("o i c -> i o c"))
+        nc.sync.dma_start(bet_sb[:, :R], bet)
         for o in range(PASSES):
             nc.sync.dma_start(word_sb[o][:].bitcast(I32), x_words[o].rearrange("p c j -> p (c j)").bitcast(I32))
 
         scale_spread = keep.tile([P, S], U8, name="scale_spread", align_bytes=64)
         nc.vector.tensor_copy(scale_spread[:], scale_sb[:].indirect(offs_sb[:]))
-        for q in range(4):
+        for base in range(0, P, QUADRANT):
             nc.sync.dma_start(
-                scale_px[32 * q : 32 * q + 4, :].bitcast(I32), scale_spread[32 * q : 32 * q + 32 : 4, :].bitcast(I32)
+                scale_px[base : base + SCALE_ROWS, :].bitcast(I32),
+                scale_spread[base : base + QUADRANT : SPREAD, :].bitcast(I32),
             )
 
         gam_px = keep.tile([P, S], F32, name="gam_px")
-        bet_px = keep.tile([P, S], F32, name="bet_px", tag="shared", align_bytes=64)
+        bet_px = keep.tile([P, S], F32, name="bet_px")
         for table, picked in ((gam_sb, gam_px), (bet_sb, bet_px)):
             for first in range(0, S, HALF):
                 entries = lab_sb[:, first // LIST_ROWS : (first + HALF) // LIST_ROWS]
@@ -100,14 +103,14 @@ def tile_picked_yspade_silu_p_kernel(tc, x_words, x_scales, w1, gam, bet, offs, 
                     stop=(o == PASSES - 1),
                 )
 
-        stats = keep.tile([P, 6 * len(banks)], F32, name="stats")
+        stats = keep.tile([P, len(banks), STATS], F32, name="stats")
         mean_var = keep.tile([P, 2], F32, name="mean_var")
         rstd = keep.tile([P, 1], F32, name="rstd")
-        nc.vector.bn_stats(stats[:, 0:6], y[0][:])
-        nc.vector.tensor_scalar_add(stats[:, 2:3], stats[:, 2:3], S * EPS)
+        nc.vector.bn_stats(stats[:, 0, :], y[0][:])
+        nc.vector.tensor_scalar_add(stats[:, 0, 2:3], stats[:, 0, 2:3], S * EPS)
         for b in range(1, len(banks)):
-            nc.vector.bn_stats(stats[:, 6 * b : 6 * b + 6], y[b][:])
-        nc.vector.bn_aggr(mean_var[:], stats[:])
+            nc.vector.bn_stats(stats[:, b, :], y[b][:])
+        nc.vector.bn_aggr(mean_var[:], stats[:].rearrange("p b s -> p (b s)"))
         nc.gpsimd.tensor_tensor(rstd[:], mean_var[:, 1:2], minus_half[:], ALU.pow)
 
         scaled = keep.tile([P, S], F32, name="scaled")

@@ -19,6 +19,7 @@ ACT = mybir.ActivationFunctionType
 P = 128
 PACK = 4
 PASSES = K // (P * PACK)
+TRIPLE = 3
 STATS = 6
 LIST_ROWS = 16
 QUADRANT = 32
@@ -50,6 +51,10 @@ def tile_picked_yspade_silu_p_kernel(tc, x_words, x_scales, w1, gam, bet, offs, 
         nc.vector.memset(gam_sb[:, R:], 0.0)
         nc.vector.memset(bet_sb[:, R:], 0.0)
         nc.vector.memset(minus_half[:], -0.5)
+        stats = keep.tile([P, TRIPLE + 3 * STATS], F32, name="stats")
+        nc.vector.memset(stats[:, :TRIPLE], 0.0)
+        nc.vector.tensor_scalar_add(stats[:, 0:1], stats[:, 0:1], 2.0**-60)
+        nc.vector.tensor_scalar_add(stats[:, 2:3], stats[:, 2:3], S * EPS)
 
         nc.sync.dma_start(gam_sb[:, :R], gam)
         nc.sync.dma_start(lab_sb[:], lab)
@@ -103,14 +108,11 @@ def tile_picked_yspade_silu_p_kernel(tc, x_words, x_scales, w1, gam, bet, offs, 
                     stop=(o == PASSES - 1),
                 )
 
-        stats = keep.tile([P, len(banks), STATS], F32, name="stats")
         mean_var = keep.tile([P, 2], F32, name="mean_var")
         rstd = keep.tile([P, 1], F32, name="rstd")
-        nc.vector.bn_stats(stats[:, 0, :], y[0][:])
-        nc.vector.tensor_scalar_add(stats[:, 0, 2:3], stats[:, 0, 2:3], S * EPS)
-        for b in range(1, len(banks)):
-            nc.vector.bn_stats(stats[:, b, :], y[b][:])
-        nc.vector.bn_aggr(mean_var[:], stats[:].rearrange("p b s -> p (b s)"))
+        for b in range(len(banks)):
+            nc.vector.bn_stats(stats[:, TRIPLE + b * STATS : TRIPLE + (b + 1) * STATS], y[b][:])
+        nc.vector.bn_aggr(mean_var[:], stats[:])
         nc.gpsimd.tensor_tensor(rstd[:], mean_var[:, 1:2], minus_half[:], ALU.pow)
 
         scaled = keep.tile([P, S], F32, name="scaled")

@@ -24,7 +24,6 @@ STATS = 6
 LIST_ROWS = 16
 QUADRANT = 32
 SCALE_ROWS = 4
-SPREAD = QUADRANT // (PASSES * SCALE_ROWS)
 HALF = S // 2
 QUARTER = S // 4
 WINDOW = R + 8
@@ -41,67 +40,79 @@ def tile_picked_yspade_silu_p_kernel(tc, x_words, x_scales, w1, gam, bet, offs, 
         gam_sb = keep.tile([P, WINDOW], F32, name="gam_sb")
         bet_sb = keep.tile([P, WINDOW], F32, name="bet_sb")
         scale_sb = keep.tile([P, T], U8, name="scale_sb", align_bytes=64)
-        word_sb = [keep.tile([P, T], U32, name="word_sb%d" % o, align_bytes=64) for o in range(PASSES)]
-        w_raw = keep.tile([P, PASSES, PACK, N], F32, name="w_raw")
-        minus_half = keep.tile([P, 1], F32, name="minus_half")
-
-        nc.vector.memset(scale_sb[:].bitcast(I32), 0)
         scale_px = keep.tile([P, PASSES * S], U8, name="scale_px", align_bytes=64)
+        word_sb = [keep.tile([P, T], U32, name="word_sb%d" % o, align_bytes=64) for o in range(PASSES)]
+        w_raw = [keep.tile([P, PACK, N], F32, name="w_raw%d" % o) for o in range(PASSES)]
+        minus_half = keep.tile([P, 1], F32, name="minus_half")
+        quarters = [slice(first, first + QUARTER) for first in range(0, S, QUARTER)]
+        stats = keep.tile([P, TRIPLE + len(quarters) * STATS], F32, name="stats")
+
+        nc.vector.memset(scale_sb[QUADRANT : 2 * QUADRANT, :].bitcast(I32), 0)
+        nc.vector.memset(scale_sb[2 * QUADRANT :, :].bitcast(I32), 0)
         nc.vector.memset(scale_px[:].bitcast(I32), 0)
         nc.vector.memset(gam_sb[:, R:], 0.0)
         nc.vector.memset(bet_sb[:, R:], 0.0)
         nc.vector.memset(minus_half[:], -0.5)
-        stats = keep.tile([P, TRIPLE + 3 * STATS], F32, name="stats")
         nc.vector.memset(stats[:, :TRIPLE], 0.0)
         nc.vector.tensor_scalar_add(stats[:, 0:1], stats[:, 0:1], 2.0**-60)
         nc.vector.tensor_scalar_add(stats[:, 2:3], stats[:, 2:3], S * EPS)
 
+        w_rows = w1.rearrange("(o p j) m -> o p j m", o=PASSES, j=PACK)
         nc.sync.dma_start(gam_sb[:, :R], gam)
         nc.sync.dma_start(lab_sb[:], lab)
         nc.sync.dma_start(offs_sb[:], offs)
-        nc.sync.dma_start(w_raw[:], w1.rearrange("(o p j) m -> p o j m", o=PASSES, j=PACK))
-        nc.sync.dma_start(scale_sb[0:P:SPREAD, :].bitcast(I32), x_scales.bitcast(I32).rearrange("o i c -> i o c"))
+        nc.sync.dma_start(scale_sb[:QUADRANT, :].bitcast(I32), x_scales.bitcast(I32).rearrange("o i c -> i o c"))
         nc.sync.dma_start(bet_sb[:, :R], bet)
-        for o in range(PASSES):
-            nc.sync.dma_start(word_sb[o][:].bitcast(I32), x_words[o].rearrange("p c j -> p (c j)").bitcast(I32))
-
-        scale_spread = keep.tile([P, S], U8, name="scale_spread", align_bytes=64)
-        nc.vector.tensor_copy(scale_spread[:], scale_sb[:].indirect(offs_sb[:]))
-        for base in range(0, P, QUADRANT):
-            nc.sync.dma_start(
-                scale_px[base : base + SCALE_ROWS, :].bitcast(I32),
-                scale_spread[base : base + QUADRANT : SPREAD, :].bitcast(I32),
-            )
+        nc.sync.dma_start(word_sb[0][:].bitcast(I32), x_words[0].rearrange("p c j -> p (c j)").bitcast(I32))
+        nc.sync.dma_start(w_raw[0][:], w_rows[0])
+        nc.sync.dma_start(word_sb[1][:].bitcast(I32), x_words[1].rearrange("p c j -> p (c j)").bitcast(I32))
+        nc.sync.dma_start(w_raw[1][:], w_rows[1])
 
         gam_px = keep.tile([P, S], F32, name="gam_px")
         bet_px = keep.tile([P, S], F32, name="bet_px")
-        for table, picked in ((gam_sb, gam_px), (bet_sb, bet_px)):
+
+        def by_region(table, picked):
             for first in range(0, S, HALF):
                 entries = lab_sb[:, first // LIST_ROWS : (first + HALF) // LIST_ROWS]
                 nc.vector.tensor_copy(picked[:, first : first + HALF], table[:].indirect(entries))
 
-        w_grouped = keep.tile([P, PASSES, N, PACK], BF16, name="w_grouped", align_bytes=64)
-        nc.scalar.copy(w_grouped[:], w_raw[:].rearrange("p o j m -> p o m j"))
-        w_codes = keep.tile([P, PASSES * N], U32, name="w_codes", align_bytes=64)
-        w_scales = keep.tile([P, PASSES * N], U8, name="w_scales", align_bytes=64)
-        nc.vector.quantize_mx(
-            out=w_codes[:].bitcast(FP8X4), scales=w_scales[:], in_=w_grouped[:].rearrange("p o m j -> p (o m j)")
-        )
+        by_region(gam_sb, gam_px)
+        scale_spread = keep.tile([P, S], U8, name="scale_spread", align_bytes=64)
+        nc.vector.tensor_copy(scale_spread[:], scale_sb[:].indirect(offs_sb[:]))
+        rows = PASSES * SCALE_ROWS
+        for q in range(P // QUADRANT):
+            nc.sync.dma_start(
+                scale_px[q * QUADRANT : q * QUADRANT + SCALE_ROWS, :].bitcast(I32),
+                scale_spread[q * rows : (q + 1) * rows, :].bitcast(I32),
+            )
+        by_region(bet_sb, bet_px)
 
         word_px = [keep.tile([P, S], U32, name="word_px%d" % o, align_bytes=64) for o in range(PASSES)]
-        nc.vector.tensor_copy(word_px[0][:], word_sb[0][:].indirect(offs_sb[:]))
-        for first in range(0, S, HALF):
-            entries = offs_sb[:, first // LIST_ROWS : (first + HALF) // LIST_ROWS]
-            nc.vector.tensor_copy(word_px[1][:, first : first + HALF], word_sb[1][:].indirect(entries))
+        w_grouped = [keep.tile([P, N, PACK], BF16, name="w_grouped%d" % o, align_bytes=64) for o in range(PASSES)]
+        w_codes = [keep.tile([P, N], U32, name="w_codes%d" % o, align_bytes=64) for o in range(PASSES)]
+        w_scales = [keep.tile([P, N], U8, name="w_scales%d" % o, align_bytes=64) for o in range(PASSES)]
 
-        banks = [slice(0, HALF), slice(HALF, HALF + QUARTER), slice(HALF + QUARTER, S)]
-        y = [psum.tile([P, cols.stop - cols.start], F32, name="y%d" % b) for b, cols in enumerate(banks)]
+        def quantise(o, cols):
+            nc.scalar.copy(w_grouped[o][:, cols, :], w_raw[o][:, :, cols].rearrange("p j m -> p m j"))
+            nc.vector.quantize_mx(
+                out=w_codes[o][:, cols].bitcast(FP8X4),
+                scales=w_scales[o][:, cols],
+                in_=w_grouped[o][:, cols, :].rearrange("p m j -> p (m j)"),
+            )
+
+        nc.vector.tensor_copy(word_px[0][:], word_sb[0][:].indirect(offs_sb[:]))
+        quantise(0, slice(0, N))
+        nc.vector.tensor_copy(word_px[1][:], word_sb[1][:].indirect(offs_sb[:]))
+        quantise(1, slice(0, N // 2))
+        quantise(1, slice(N // 2, N))
+
+        y = [psum.tile([P, QUARTER], F32, name="y%d" % b) for b in range(len(quarters))]
         for o in range(PASSES):
-            for b, cols in enumerate(banks):
+            for b, cols in enumerate(quarters):
                 nc.tensor.matmul_mx(
                     out=y[b][:],
-                    lhsT=w_codes[:, o * N : (o + 1) * N].bitcast(FP8X4),
-                    lhsT_scale=w_scales[:, o * N : (o + 1) * N],
+                    lhsT=w_codes[o][:].bitcast(FP8X4),
+                    lhsT_scale=w_scales[o][:],
                     rhs=word_px[o][:, cols].bitcast(FP8X4),
                     rhs_scale=scale_px[:, o * S + cols.start : o * S + cols.stop],
                     start=(o == 0),
@@ -110,7 +121,7 @@ def tile_picked_yspade_silu_p_kernel(tc, x_words, x_scales, w1, gam, bet, offs, 
 
         mean_var = keep.tile([P, 2], F32, name="mean_var")
         rstd = keep.tile([P, 1], F32, name="rstd")
-        for b in range(len(banks)):
+        for b in range(len(quarters)):
             nc.vector.bn_stats(stats[:, TRIPLE + b * STATS : TRIPLE + (b + 1) * STATS], y[b][:])
         nc.vector.bn_aggr(mean_var[:], stats[:])
         nc.gpsimd.tensor_tensor(rstd[:], mean_var[:, 1:2], minus_half[:], ALU.pow)
@@ -118,14 +129,15 @@ def tile_picked_yspade_silu_p_kernel(tc, x_words, x_scales, w1, gam, bet, offs, 
         scaled = keep.tile([P, S], F32, name="scaled")
         shifted = keep.tile([P, S], F32, name="shifted")
         result = keep.tile([P, S], F32, name="result")
-        for b, cols in enumerate(banks):
+        for b, cols in enumerate(quarters):
             nc.vector.scalar_tensor_tensor(
                 scaled[:, cols], y[b][:], mean_var[:, 0:1], gam_px[:, cols], ALU.subtract, ALU.mult
             )
-        for first in range(0, S, QUARTER):
-            cols = slice(first, first + QUARTER)
+        for b, cols in enumerate(quarters):
             nc.vector.scalar_tensor_tensor(
                 shifted[:, cols], scaled[:, cols], rstd[:], bet_px[:, cols], ALU.mult, ALU.add
             )
             nc.scalar.activation(result[:, cols], shifted[:, cols], ACT.Silu)
-            nc.sync.dma_start(out[:, cols], result[:, cols])
+            if b > 0:
+                stored = slice(0, HALF) if b == 1 else cols
+                nc.sync.dma_start(out[:, stored], result[:, stored])

@@ -19,85 +19,90 @@ ACT = mybir.ActivationFunctionType
 P = 128
 PACK = 4
 PASSES = K // (P * PACK)
-TRIPLE = 3
-STATS = 6
+LINE = 4
 LIST_ROWS = 16
 QUADRANT = 32
 SCALE_ROWS = 4
+TRIPLE = 3
+STATS = 2 * TRIPLE
+NO_WEIGHT = 2.0**-60
 HALF = S // 2
 QUARTER = S // 4
-WINDOW = R + 8
+GAM_WINDOW = R + 8
+LONG = 160
+SHORT = HALF - LONG
 
 
 def tile_picked_yspade_silu_p_kernel(tc, x_words, x_scales, w1, gam, bet, offs, lab, out):
     nc = tc.nc
+    halves = [slice(first, first + HALF) for first in range(0, S, HALF)]
+    quarters = [slice(first, first + QUARTER) for first in range(0, S, QUARTER)]
     with ExitStack() as ctx:
         keep = ctx.enter_context(tc.tile_pool(name="keep", bufs=1))
         psum = ctx.enter_context(tc.psum_pool(name="psum", bufs=1))
 
         offs_sb = keep.tile([P, S // LIST_ROWS], U16, name="offs_sb")
         lab_sb = keep.tile([P, S // LIST_ROWS], U16, name="lab_sb")
-        gam_sb = keep.tile([P, WINDOW], F32, name="gam_sb")
-        bet_sb = keep.tile([P, WINDOW], F32, name="bet_sb")
-        scale_sb = keep.tile([P, T], U8, name="scale_sb", align_bytes=64)
+        gam_sb = keep.tile([P, GAM_WINDOW], F32, name="gam_sb")
+        scale_sb = keep.tile([P, T], U8, name="scale_sb", tag="table", align_bytes=64)
         scale_px = keep.tile([P, PASSES * S], U8, name="scale_px", align_bytes=64)
         word_sb = [keep.tile([P, T], U32, name="word_sb%d" % o, align_bytes=64) for o in range(PASSES)]
-        w_raw = [keep.tile([P, PACK, N], F32, name="w_raw%d" % o) for o in range(PASSES)]
+        w_raw = [keep.tile([P, PACK, N], F32, name="w_raw%d" % o, tag="w_raw%d" % o) for o in range(PASSES)]
         minus_half = keep.tile([P, 1], F32, name="minus_half")
-        quarters = [slice(first, first + QUARTER) for first in range(0, S, QUARTER)]
-        stats = keep.tile([P, TRIPLE + len(quarters) * STATS], F32, name="stats")
 
         nc.vector.memset(scale_sb[QUADRANT : 2 * QUADRANT, :].bitcast(I32), 0)
         nc.vector.memset(scale_sb[2 * QUADRANT :, :].bitcast(I32), 0)
         nc.vector.memset(scale_px[:].bitcast(I32), 0)
         nc.vector.memset(gam_sb[:, R:], 0.0)
-        nc.vector.memset(bet_sb[:, R:], 0.0)
         nc.vector.memset(minus_half[:], -0.5)
-        nc.vector.memset(stats[:, :TRIPLE], 0.0)
-        nc.vector.tensor_scalar_add(stats[:, 0:1], stats[:, 0:1], 2.0**-60)
-        nc.vector.tensor_scalar_add(stats[:, 2:3], stats[:, 2:3], S * EPS)
 
         w_rows = w1.rearrange("(o p j) m -> o p j m", o=PASSES, j=PACK)
         nc.sync.dma_start(gam_sb[:, :R], gam)
         nc.sync.dma_start(lab_sb[:], lab)
         nc.sync.dma_start(offs_sb[:], offs)
         nc.sync.dma_start(scale_sb[:QUADRANT, :].bitcast(I32), x_scales.bitcast(I32).rearrange("o i c -> i o c"))
-        nc.sync.dma_start(bet_sb[:, :R], bet)
-        nc.sync.dma_start(word_sb[0][:].bitcast(I32), x_words[0].rearrange("p c j -> p (c j)").bitcast(I32))
-        nc.sync.dma_start(w_raw[0][:], w_rows[0])
-        nc.sync.dma_start(word_sb[1][:].bitcast(I32), x_words[1].rearrange("p c j -> p (c j)").bitcast(I32))
-        nc.sync.dma_start(w_raw[1][:], w_rows[1])
+        for o in range(PASSES):
+            nc.sync.dma_start(word_sb[o][:].bitcast(I32), x_words[o].rearrange("p c j -> p (c j)").bitcast(I32))
+            nc.sync.dma_start(w_raw[o][:], w_rows[o])
+
+        def by_region(picked, window, first, count):
+            entries = lab_sb[:, first // LIST_ROWS : (first + count) // LIST_ROWS]
+            nc.vector.tensor_copy(picked, window.indirect(entries))
 
         gam_px = keep.tile([P, S], F32, name="gam_px")
-        bet_px = keep.tile([P, S], F32, name="bet_px")
+        for cols in halves:
+            by_region(gam_px[:, cols], gam_sb[:], cols.start, HALF)
 
-        def by_region(table, picked):
-            for first in range(0, S, HALF):
-                entries = lab_sb[:, first // LIST_ROWS : (first + HALF) // LIST_ROWS]
-                nc.vector.tensor_copy(picked[:, first : first + HALF], table[:].indirect(entries))
-
-        by_region(gam_sb, gam_px)
-        scale_spread = keep.tile([P, S], U8, name="scale_spread", align_bytes=64)
-        nc.vector.tensor_copy(scale_spread[:], scale_sb[:].indirect(offs_sb[:]))
+        scale_picked = keep.tile([P, S], U8, name="scale_picked", align_bytes=64)
+        nc.vector.tensor_copy(scale_picked[:], scale_sb[:].indirect(offs_sb[:]))
         rows = PASSES * SCALE_ROWS
         for q in range(P // QUADRANT):
             nc.sync.dma_start(
                 scale_px[q * QUADRANT : q * QUADRANT + SCALE_ROWS, :].bitcast(I32),
-                scale_spread[q * rows : (q + 1) * rows, :].bitcast(I32),
+                scale_picked[q * rows : (q + 1) * rows, :].bitcast(I32),
             )
-        by_region(bet_sb, bet_px)
+
+        bet_sb = keep.tile([P, R + TRIPLE + len(halves) * STATS], F32, name="bet_sb", tag="table", align_bytes=64)
+        nc.sync.dma_start(bet_sb[:, :R], bet)
+        stats = bet_sb[:, R:]
+        nc.vector.memset(stats, 0.0)
+        nc.vector.tensor_scalar_add(stats[:, 0:1], stats[:, 0:1], NO_WEIGHT)
+        nc.vector.tensor_scalar_add(stats[:, 2:3], stats[:, 2:3], S * EPS)
 
         word_px = [keep.tile([P, S], U32, name="word_px%d" % o, align_bytes=64) for o in range(PASSES)]
         w_grouped = [keep.tile([P, N, PACK], BF16, name="w_grouped%d" % o, align_bytes=64) for o in range(PASSES)]
         w_codes = [keep.tile([P, N], U32, name="w_codes%d" % o, align_bytes=64) for o in range(PASSES)]
         w_scales = [keep.tile([P, N], U8, name="w_scales%d" % o, align_bytes=64) for o in range(PASSES)]
 
-        def quantise(o, cols):
-            nc.scalar.copy(w_grouped[o][:, cols, :], w_raw[o][:, :, cols].rearrange("p j m -> p m j"))
+        def quantise(o, features):
+            nc.scalar.copy(
+                w_grouped[o][:, features, :].rearrange("p (c i) j -> p c j i", i=LINE),
+                w_raw[o][:, :, features].rearrange("p j (c i) -> p c j i", i=LINE),
+            )
             nc.vector.quantize_mx(
-                out=w_codes[o][:, cols].bitcast(FP8X4),
-                scales=w_scales[o][:, cols],
-                in_=w_grouped[o][:, cols, :].rearrange("p m j -> p (m j)"),
+                out=w_codes[o][:, features].bitcast(FP8X4),
+                scales=w_scales[o][:, features],
+                in_=w_grouped[o][:, features, :].rearrange("p m j -> p (m j)"),
             )
 
         nc.vector.tensor_copy(word_px[0][:], word_sb[0][:].indirect(offs_sb[:]))
@@ -106,11 +111,15 @@ def tile_picked_yspade_silu_p_kernel(tc, x_words, x_scales, w1, gam, bet, offs, 
         quantise(1, slice(0, N // 2))
         quantise(1, slice(N // 2, N))
 
-        y = [psum.tile([P, QUARTER], F32, name="y%d" % b) for b in range(len(quarters))]
+        bet_px = keep.tile([P, S], F32, name="bet_px", tag="w_raw1")
+        by_region(bet_px[:, :LONG], bet_sb[:], 0, LONG)
+        by_region(bet_px[:, LONG : 2 * LONG], bet_sb[:, :R], LONG, LONG)
+
+        y = [psum.tile([P, HALF], F32, name="y%d" % h) for h in range(len(halves))]
         for o in range(PASSES):
-            for b, cols in enumerate(quarters):
+            for h, cols in enumerate(halves):
                 nc.tensor.matmul_mx(
-                    out=y[b][:],
+                    out=y[h][:],
                     lhsT=w_codes[o][:].bitcast(FP8X4),
                     lhsT_scale=w_scales[o][:],
                     rhs=word_px[o][:, cols].bitcast(FP8X4),
@@ -121,23 +130,25 @@ def tile_picked_yspade_silu_p_kernel(tc, x_words, x_scales, w1, gam, bet, offs, 
 
         mean_var = keep.tile([P, 2], F32, name="mean_var")
         rstd = keep.tile([P, 1], F32, name="rstd")
-        for b in range(len(quarters)):
-            nc.vector.bn_stats(stats[:, TRIPLE + b * STATS : TRIPLE + (b + 1) * STATS], y[b][:])
-        nc.vector.bn_aggr(mean_var[:], stats[:])
+        for h in range(len(halves)):
+            nc.vector.bn_stats(stats[:, TRIPLE + h * STATS : TRIPLE + (h + 1) * STATS], y[h][:])
+        by_region(bet_px[:, 2 * LONG : S - SHORT], bet_sb[:, : R + TRIPLE + STATS], 2 * LONG, SHORT)
+        nc.vector.bn_aggr(mean_var[:], stats)
+        by_region(bet_px[:, S - SHORT :], bet_sb[:], S - SHORT, SHORT)
         nc.gpsimd.tensor_tensor(rstd[:], mean_var[:, 1:2], minus_half[:], ALU.pow)
 
         scaled = keep.tile([P, S], F32, name="scaled")
         shifted = keep.tile([P, S], F32, name="shifted")
         result = keep.tile([P, S], F32, name="result")
-        for b, cols in enumerate(quarters):
+        for h, cols in enumerate(halves):
             nc.vector.scalar_tensor_tensor(
-                scaled[:, cols], y[b][:], mean_var[:, 0:1], gam_px[:, cols], ALU.subtract, ALU.mult
+                scaled[:, cols], y[h][:], mean_var[:, 0:1], gam_px[:, cols], ALU.subtract, ALU.mult
             )
-        for b, cols in enumerate(quarters):
+        stores = {HALF: halves[0], HALF + QUARTER: quarters[2], S: quarters[3]}
+        for cols in quarters:
             nc.vector.scalar_tensor_tensor(
                 shifted[:, cols], scaled[:, cols], rstd[:], bet_px[:, cols], ALU.mult, ALU.add
             )
             nc.scalar.activation(result[:, cols], shifted[:, cols], ACT.Silu)
-            if b > 0:
-                stored = slice(0, HALF) if b == 1 else cols
-                nc.sync.dma_start(out[:, stored], result[:, stored])
+            if cols.stop in stores:
+                nc.sync.dma_start(out[:, stores[cols.stop]], result[:, stores[cols.stop]])

@@ -23,6 +23,7 @@ LINE = 4
 LIST_ROWS = 16
 QUADRANT = 32
 SCALE_ROWS = 4
+SPREAD = QUADRANT // (PASSES * SCALE_ROWS)
 TRIPLE = 3
 STATS = 2 * TRIPLE
 NO_WEIGHT = 2.0**-60
@@ -50,8 +51,7 @@ def tile_picked_yspade_silu_p_kernel(tc, x_words, x_scales, w1, gam, bet, offs, 
         w_raw = [keep.tile([P, PACK, N], F32, name="w_raw%d" % o, tag="w_raw%d" % o) for o in range(PASSES)]
         minus_half = keep.tile([P, 1], F32, name="minus_half")
 
-        nc.vector.memset(scale_sb[QUADRANT : 2 * QUADRANT, :].bitcast(I32), 0)
-        nc.vector.memset(scale_sb[2 * QUADRANT :, :].bitcast(I32), 0)
+        nc.vector.memset(scale_sb[:].bitcast(I32), 0)
         nc.vector.memset(scale_px[:].bitcast(I32), 0)
         nc.vector.memset(gam_sb[:, R:], 0.0)
         nc.vector.memset(minus_half[:], -0.5)
@@ -60,10 +60,11 @@ def tile_picked_yspade_silu_p_kernel(tc, x_words, x_scales, w1, gam, bet, offs, 
         nc.sync.dma_start(gam_sb[:, :R], gam)
         nc.sync.dma_start(lab_sb[:], lab)
         nc.sync.dma_start(offs_sb[:], offs)
-        nc.sync.dma_start(scale_sb[:QUADRANT, :].bitcast(I32), x_scales.bitcast(I32).rearrange("o i c -> i o c"))
+        nc.sync.dma_start(w_raw[0][:], w_rows[0])
+        nc.sync.dma_start(scale_sb[0:P:SPREAD, :].bitcast(I32), x_scales.bitcast(I32).rearrange("o i c -> i o c"))
         for o in range(PASSES):
             nc.sync.dma_start(word_sb[o][:].bitcast(I32), x_words[o].rearrange("p c j -> p (c j)").bitcast(I32))
-            nc.sync.dma_start(w_raw[o][:], w_rows[o])
+        nc.sync.dma_start(w_raw[1][:], w_rows[1])
 
         def by_region(picked, window, first, count):
             entries = lab_sb[:, first // LIST_ROWS : (first + count) // LIST_ROWS]
@@ -75,11 +76,10 @@ def tile_picked_yspade_silu_p_kernel(tc, x_words, x_scales, w1, gam, bet, offs, 
 
         scale_picked = keep.tile([P, S], U8, name="scale_picked", align_bytes=64)
         nc.vector.tensor_copy(scale_picked[:], scale_sb[:].indirect(offs_sb[:]))
-        rows = PASSES * SCALE_ROWS
-        for q in range(P // QUADRANT):
+        for base in range(0, P, QUADRANT):
             nc.sync.dma_start(
-                scale_px[q * QUADRANT : q * QUADRANT + SCALE_ROWS, :].bitcast(I32),
-                scale_picked[q * rows : (q + 1) * rows, :].bitcast(I32),
+                scale_px[base : base + SCALE_ROWS, :].bitcast(I32),
+                scale_picked[base : base + QUADRANT : SPREAD, :].bitcast(I32),
             )
 
         bet_sb = keep.tile([P, R + TRIPLE + len(halves) * STATS], F32, name="bet_sb", tag="table", align_bytes=64)

@@ -94,11 +94,13 @@ def tile_picked_yspade_silu_p_kernel(tc, x_words, x_scales, w1, gam, bet, offs, 
         w_codes = [keep.tile([P, N], U32, name="w_codes%d" % o, align_bytes=64) for o in range(PASSES)]
         w_scales = [keep.tile([P, N], U8, name="w_scales%d" % o, align_bytes=64) for o in range(PASSES)]
 
-        def quantise(o, features):
-            nc.scalar.copy(
+        def round_to_bf16(copy, o, features):
+            copy(
                 w_grouped[o][:, features, :].rearrange("p (c i) j -> p c j i", i=LINE),
                 w_raw[o][:, :, features].rearrange("p j (c i) -> p c j i", i=LINE),
             )
+
+        def quantise(o, features):
             nc.vector.quantize_mx(
                 out=w_codes[o][:, features].bitcast(FP8X4),
                 scales=w_scales[o][:, features],
@@ -106,9 +108,13 @@ def tile_picked_yspade_silu_p_kernel(tc, x_words, x_scales, w1, gam, bet, offs, 
             )
 
         nc.vector.tensor_copy(word_px[0][:], word_sb[0][:].indirect(offs_sb[:]))
+        round_to_bf16(nc.scalar.copy, 0, slice(0, N))
         quantise(0, slice(0, N))
         nc.vector.tensor_copy(word_px[1][:], word_sb[1][:].indirect(offs_sb[:]))
+        round_to_bf16(nc.scalar.copy, 1, slice(0, N // 2))
         quantise(1, slice(0, N // 2))
+        round_to_bf16(nc.scalar.copy, 1, slice(N // 2, 3 * N // 4))
+        round_to_bf16(nc.gpsimd.tensor_copy, 1, slice(3 * N // 4, N))
         quantise(1, slice(N // 2, N))
 
         bet_px = keep.tile([P, S], F32, name="bet_px", tag="w_raw1")

@@ -27,52 +27,45 @@ SPREAD = QUADRANT // (PASSES * SCALE_ROWS)
 TRIPLE = 3
 STATS = 2 * TRIPLE
 NO_WEIGHT = 2.0**-60
-HALF = S // 2
 QUARTER = S // 4
-GAM_WINDOW = R + 8
-LONG = 160
-SHORT = HALF - LONG
 
 
 def tile_picked_yspade_silu_p_kernel(tc, x_words, x_scales, w1, gam, bet, offs, lab, out):
     nc = tc.nc
-    halves = [slice(first, first + HALF) for first in range(0, S, HALF)]
     quarters = [slice(first, first + QUARTER) for first in range(0, S, QUARTER)]
+    banks = [slice(0, 2 * QUARTER), quarters[2], quarters[3]]
     with ExitStack() as ctx:
         keep = ctx.enter_context(tc.tile_pool(name="keep", bufs=1))
+        tables = ctx.enter_context(tc.tile_pool(name="tables", bufs=1))
         psum = ctx.enter_context(tc.psum_pool(name="psum", bufs=1))
 
         offs_sb = keep.tile([P, S // LIST_ROWS], U16, name="offs_sb")
         lab_sb = keep.tile([P, S // LIST_ROWS], U16, name="lab_sb")
-        gam_sb = keep.tile([P, GAM_WINDOW], F32, name="gam_sb")
-        scale_sb = keep.tile([P, T], U8, name="scale_sb", tag="table", align_bytes=64)
+        scale_sb = tables.tile([P, T], U8, name="scale_sb", offset=0)
         scale_px = keep.tile([P, PASSES * S], U8, name="scale_px", align_bytes=64)
         word_sb = [keep.tile([P, T], U32, name="word_sb%d" % o, align_bytes=64) for o in range(PASSES)]
-        w_raw = [keep.tile([P, PACK, N], F32, name="w_raw%d" % o, tag="w_raw%d" % o) for o in range(PASSES)]
+        w_raw = [keep.tile([P, PACK, N], F32, name="w_raw%d" % o) for o in range(PASSES)]
         minus_half = keep.tile([P, 1], F32, name="minus_half")
+        stats = keep.tile([P, TRIPLE + len(banks) * STATS], F32, name="stats")
 
         nc.vector.memset(scale_sb[:].bitcast(I32), 0)
         nc.vector.memset(scale_px[:].bitcast(I32), 0)
-        nc.vector.memset(gam_sb[:, R:], 0.0)
         nc.vector.memset(minus_half[:], -0.5)
+        nc.vector.memset(stats[:, :TRIPLE], 0.0)
+        nc.vector.tensor_scalar_add(stats[:, 0:1], stats[:, 0:1], NO_WEIGHT)
+        nc.vector.tensor_scalar_add(stats[:, 2:3], stats[:, 2:3], S * EPS)
+
+        unread = keep.tile([P, 1], F32, name="unread")
+        nc.scalar.activation(unread[:], minus_half[:], ACT.Silu)
 
         w_rows = w1.rearrange("(o p j) m -> o p j m", o=PASSES, j=PACK)
-        nc.sync.dma_start(gam_sb[:, :R], gam)
-        nc.sync.dma_start(lab_sb[:], lab)
+        for o in range(PASSES):
+            nc.sync.dma_start(w_raw[o][:], w_rows[o])
         nc.sync.dma_start(offs_sb[:], offs)
-        nc.sync.dma_start(w_raw[0][:], w_rows[0])
         nc.sync.dma_start(scale_sb[0:P:SPREAD, :].bitcast(I32), x_scales.bitcast(I32).rearrange("o i c -> i o c"))
         for o in range(PASSES):
             nc.sync.dma_start(word_sb[o][:].bitcast(I32), x_words[o].rearrange("p c j -> p (c j)").bitcast(I32))
-        nc.sync.dma_start(w_raw[1][:], w_rows[1])
-
-        def by_region(picked, window, first, count):
-            entries = lab_sb[:, first // LIST_ROWS : (first + count) // LIST_ROWS]
-            nc.vector.tensor_copy(picked, window.indirect(entries))
-
-        gam_px = keep.tile([P, S], F32, name="gam_px")
-        for cols in halves:
-            by_region(gam_px[:, cols], gam_sb[:], cols.start, HALF)
+        nc.sync.dma_start(lab_sb[:], lab)
 
         scale_picked = keep.tile([P, S], U8, name="scale_picked", align_bytes=64)
         nc.vector.tensor_copy(scale_picked[:], scale_sb[:].indirect(offs_sb[:]))
@@ -82,48 +75,43 @@ def tile_picked_yspade_silu_p_kernel(tc, x_words, x_scales, w1, gam, bet, offs, 
                 scale_picked[base : base + QUADRANT : SPREAD, :].bitcast(I32),
             )
 
-        bet_sb = keep.tile([P, R + TRIPLE + len(halves) * STATS], F32, name="bet_sb", tag="table", align_bytes=64)
-        nc.sync.dma_start(bet_sb[:, :R], bet)
-        stats = bet_sb[:, R:]
-        nc.vector.memset(stats, 0.0)
-        nc.vector.tensor_scalar_add(stats[:, 0:1], stats[:, 0:1], NO_WEIGHT)
-        nc.vector.tensor_scalar_add(stats[:, 2:3], stats[:, 2:3], S * EPS)
+        gam_sb = tables.tile([P, R], F32, name="gam_sb", offset=0)
+        bet_sb = tables.tile([P, R], F32, name="bet_sb", offset=4 * R)
+        nc.sync.dma_start(gam_sb[:], gam)
+        nc.sync.dma_start(bet_sb[:], bet)
 
         word_px = [keep.tile([P, S], U32, name="word_px%d" % o, align_bytes=64) for o in range(PASSES)]
         w_grouped = [keep.tile([P, N, PACK], BF16, name="w_grouped%d" % o, align_bytes=64) for o in range(PASSES)]
         w_codes = [keep.tile([P, N], U32, name="w_codes%d" % o, align_bytes=64) for o in range(PASSES)]
         w_scales = [keep.tile([P, N], U8, name="w_scales%d" % o, align_bytes=64) for o in range(PASSES)]
 
-        def round_to_bf16(copy, o, features):
-            copy(
-                w_grouped[o][:, features, :].rearrange("p (c i) j -> p c j i", i=LINE),
-                w_raw[o][:, :, features].rearrange("p j (c i) -> p c j i", i=LINE),
+        for o in range(PASSES):
+            nc.scalar.copy(
+                w_grouped[o][:].rearrange("p (c i) j -> p c j i", i=LINE),
+                w_raw[o][:].rearrange("p j (c i) -> p c j i", i=LINE),
+            )
+            nc.vector.quantize_mx(
+                out=w_codes[o][:].bitcast(FP8X4),
+                scales=w_scales[o][:],
+                in_=w_grouped[o][:].rearrange("p m j -> p (m j)"),
             )
 
-        def quantise(o, features):
-            nc.vector.quantize_mx(
-                out=w_codes[o][:, features].bitcast(FP8X4),
-                scales=w_scales[o][:, features],
-                in_=w_grouped[o][:, features, :].rearrange("p m j -> p (m j)"),
-            )
+        def entries(table, cols):
+            return table[:, cols.start // LIST_ROWS : cols.stop // LIST_ROWS]
 
         nc.vector.tensor_copy(word_px[0][:], word_sb[0][:].indirect(offs_sb[:]))
-        round_to_bf16(nc.scalar.copy, 0, slice(0, N))
-        quantise(0, slice(0, N))
-        nc.vector.tensor_copy(word_px[1][:], word_sb[1][:].indirect(offs_sb[:]))
-        round_to_bf16(nc.scalar.copy, 1, slice(0, N // 2))
-        quantise(1, slice(0, N // 2))
-        round_to_bf16(nc.scalar.copy, 1, slice(N // 2, 3 * N // 4))
-        round_to_bf16(nc.gpsimd.tensor_copy, 1, slice(3 * N // 4, N))
-        quantise(1, slice(N // 2, N))
+        for cols in banks:
+            nc.vector.tensor_copy(word_px[1][:, cols], word_sb[1][:].indirect(entries(offs_sb, cols)))
 
-        bet_px = keep.tile([P, S], F32, name="bet_px", tag="w_raw1")
-        by_region(bet_px[:, :LONG], bet_sb[:], 0, LONG)
-        by_region(bet_px[:, LONG : 2 * LONG], bet_sb[:, :R], LONG, LONG)
+        gam_px = keep.tile([P, S], F32, name="gam_px")
+        bet_px = keep.tile([P, S], F32, name="bet_px")
+        for picked, table in ((gam_px, gam_sb), (bet_px, bet_sb)):
+            for cols in quarters:
+                nc.scalar.activation(picked[:, cols], table[:].indirect(entries(lab_sb, cols)), ACT.Copy)
 
-        y = [psum.tile([P, HALF], F32, name="y%d" % h) for h in range(len(halves))]
+        y = [psum.tile([P, cols.stop - cols.start], F32, name="y%d" % h) for h, cols in enumerate(banks)]
         for o in range(PASSES):
-            for h, cols in enumerate(halves):
+            for h, cols in enumerate(banks):
                 nc.tensor.matmul_mx(
                     out=y[h][:],
                     lhsT=w_codes[o][:].bitcast(FP8X4),
@@ -136,21 +124,19 @@ def tile_picked_yspade_silu_p_kernel(tc, x_words, x_scales, w1, gam, bet, offs, 
 
         mean_var = keep.tile([P, 2], F32, name="mean_var")
         rstd = keep.tile([P, 1], F32, name="rstd")
-        for h in range(len(halves)):
+        for h in range(len(banks)):
             nc.vector.bn_stats(stats[:, TRIPLE + h * STATS : TRIPLE + (h + 1) * STATS], y[h][:])
-        by_region(bet_px[:, 2 * LONG : S - SHORT], bet_sb[:, : R + TRIPLE + STATS], 2 * LONG, SHORT)
-        nc.vector.bn_aggr(mean_var[:], stats)
-        by_region(bet_px[:, S - SHORT :], bet_sb[:], S - SHORT, SHORT)
+        nc.vector.bn_aggr(mean_var[:], stats[:])
         nc.gpsimd.tensor_tensor(rstd[:], mean_var[:, 1:2], minus_half[:], ALU.pow)
 
         scaled = keep.tile([P, S], F32, name="scaled")
         shifted = keep.tile([P, S], F32, name="shifted")
         result = keep.tile([P, S], F32, name="result")
-        for h, cols in enumerate(halves):
+        for h, cols in enumerate(banks):
             nc.vector.scalar_tensor_tensor(
                 scaled[:, cols], y[h][:], mean_var[:, 0:1], gam_px[:, cols], ALU.subtract, ALU.mult
             )
-        stores = {HALF: halves[0], HALF + QUARTER: quarters[2], S: quarters[3]}
+        stores = {2 * QUARTER: slice(0, 2 * QUARTER), 3 * QUARTER: quarters[2], S: quarters[3]}
         for cols in quarters:
             nc.vector.scalar_tensor_tensor(
                 shifted[:, cols], scaled[:, cols], rstd[:], bet_px[:, cols], ALU.mult, ALU.add

@@ -136,7 +136,7 @@ def tile_picked_yspade_silu_p_kernel(tc, x_words, x_scales, w1, gam, bet, offs, 
             nc.vector.scalar_tensor_tensor(
                 scaled[:, cols], y[h][:], mean_var[:, 0:1], gam_px[:, cols], ALU.subtract, ALU.mult
             )
-        stores = {2 * QUARTER: slice(0, 2 * QUARTER), 3 * QUARTER: quarters[2], S: quarters[3]}
+        stores = {QUARTER: quarters[0], 2 * QUARTER: quarters[1], S: slice(2 * QUARTER, S)}
         for cols in quarters:
             nc.vector.scalar_tensor_tensor(
                 shifted[:, cols], scaled[:, cols], rstd[:], bet_px[:, cols], ALU.mult, ALU.add

@@ -20,6 +20,7 @@ P = 128
 PACK = 4
 PASSES = K // (P * PACK)
 LINE = 4
+BURST = 256
 LIST_ROWS = 16
 QUADRANT = 32
 SCALE_ROWS = 4
@@ -41,10 +42,10 @@ def tile_picked_yspade_silu_p_kernel(tc, x_words, x_scales, w1, gam, bet, offs, 
 
         offs_sb = keep.tile([P, S // LIST_ROWS], U16, name="offs_sb")
         lab_sb = keep.tile([P, S // LIST_ROWS], U16, name="lab_sb")
-        scale_sb = tables.tile([P, T], U8, name="scale_sb", offset=0)
+        scale_sb = tables.tile([P, T], U8, name="scale_sb", offset=0, align_bytes=BURST)
         scale_px = keep.tile([P, PASSES * S], U8, name="scale_px", align_bytes=64)
-        word_sb = [keep.tile([P, T], U32, name="word_sb%d" % o, align_bytes=64) for o in range(PASSES)]
-        w_raw = [keep.tile([P, PACK, N], F32, name="w_raw%d" % o) for o in range(PASSES)]
+        word_sb = [keep.tile([P, T], U32, name="word_sb%d" % o, align_bytes=BURST) for o in range(PASSES)]
+        w_raw = [keep.tile([P, PACK, N], F32, name="w_raw%d" % o, align_bytes=BURST) for o in range(PASSES)]
         minus_half = keep.tile([P, 1], F32, name="minus_half")
         stats = keep.tile([P, TRIPLE + len(banks) * STATS], F32, name="stats")
 
@@ -75,8 +76,8 @@ def tile_picked_yspade_silu_p_kernel(tc, x_words, x_scales, w1, gam, bet, offs, 
                 scale_picked[base : base + QUADRANT : SPREAD, :].bitcast(I32),
             )
 
-        gam_sb = tables.tile([P, R], F32, name="gam_sb", offset=0)
-        bet_sb = tables.tile([P, R], F32, name="bet_sb", offset=4 * R)
+        gam_sb = tables.tile([P, R], F32, name="gam_sb", offset=0, align_bytes=BURST)
+        bet_sb = tables.tile([P, R], F32, name="bet_sb", offset=4 * R, align_bytes=BURST)
         nc.sync.dma_start(gam_sb[:], gam)
         nc.sync.dma_start(bet_sb[:], bet)
 
@@ -131,7 +132,7 @@ def tile_picked_yspade_silu_p_kernel(tc, x_words, x_scales, w1, gam, bet, offs, 
 
         scaled = keep.tile([P, S], F32, name="scaled")
         shifted = keep.tile([P, S], F32, name="shifted")
-        result = keep.tile([P, S], F32, name="result")
+        result = keep.tile([P, S], F32, name="result", align_bytes=BURST)
         for h, cols in enumerate(banks):
             nc.vector.scalar_tensor_tensor(
                 scaled[:, cols], y[h][:], mean_var[:, 0:1], gam_px[:, cols], ALU.subtract, ALU.mult

@@ -28,6 +28,7 @@ SPREAD = QUADRANT // (PASSES * SCALE_ROWS)
 TRIPLE = 3
 STATS = 2 * TRIPLE
 NO_WEIGHT = 2.0**-60
+SCALE_AT = 4 * R - BURST
 QUARTER = S // 4
 
 
@@ -42,14 +43,15 @@ def tile_picked_yspade_silu_p_kernel(tc, x_words, x_scales, w1, gam, bet, offs, 
 
         offs_sb = keep.tile([P, S // LIST_ROWS], U16, name="offs_sb")
         lab_sb = keep.tile([P, S // LIST_ROWS], U16, name="lab_sb")
-        scale_sb = tables.tile([P, T], U8, name="scale_sb", offset=0, align_bytes=BURST)
+        scale_sb = tables.tile([P, T], U8, name="scale_sb", offset=SCALE_AT, align_bytes=BURST)
         scale_px = keep.tile([P, PASSES * S], U8, name="scale_px", align_bytes=64)
         word_sb = [keep.tile([P, T], U32, name="word_sb%d" % o, align_bytes=BURST) for o in range(PASSES)]
-        w_raw = [keep.tile([P, PACK, N], F32, name="w_raw%d" % o, align_bytes=BURST) for o in range(PASSES)]
+        w_raw = keep.tile([P, PASSES, PACK * N], F32, name="w_raw", align_bytes=BURST)
         minus_half = keep.tile([P, 1], F32, name="minus_half")
         stats = keep.tile([P, TRIPLE + len(banks) * STATS], F32, name="stats")
 
-        nc.vector.memset(scale_sb[:].bitcast(I32), 0)
+        nc.vector.memset(scale_sb[:, : T // 2].bitcast(I32), 0)
+        nc.gpsimd.memset(scale_sb[:, T // 2 :].bitcast(I32), 0)
         nc.vector.memset(scale_px[:].bitcast(I32), 0)
         nc.vector.memset(minus_half[:], -0.5)
         nc.vector.memset(stats[:, :TRIPLE], 0.0)
@@ -59,9 +61,7 @@ def tile_picked_yspade_silu_p_kernel(tc, x_words, x_scales, w1, gam, bet, offs, 
         unread = keep.tile([P, 1], F32, name="unread")
         nc.scalar.activation(unread[:], minus_half[:], ACT.Silu)
 
-        w_rows = w1.rearrange("(o p j) m -> o p j m", o=PASSES, j=PACK)
-        for o in range(PASSES):
-            nc.sync.dma_start(w_raw[o][:], w_rows[o])
+        nc.sync.dma_start(w_raw[:], w1.rearrange("(o p j) m -> p o (j m)", o=PASSES, j=PACK))
         nc.sync.dma_start(offs_sb[:], offs)
         nc.sync.dma_start(scale_sb[0:P:SPREAD, :].bitcast(I32), x_scales.bitcast(I32).rearrange("o i c -> i o c"))
         for o in range(PASSES):
@@ -76,20 +76,23 @@ def tile_picked_yspade_silu_p_kernel(tc, x_words, x_scales, w1, gam, bet, offs, 
                 scale_picked[base : base + QUADRANT : SPREAD, :].bitcast(I32),
             )
 
-        gam_sb = tables.tile([P, R], F32, name="gam_sb", offset=0, align_bytes=BURST)
-        bet_sb = tables.tile([P, R], F32, name="bet_sb", offset=4 * R, align_bytes=BURST)
+        gam_sb = tables.tile([P, R], F32, name="gam_sb", offset=SCALE_AT + BURST - 4 * R, align_bytes=BURST)
+        bet_sb = tables.tile([P, R], F32, name="bet_sb", offset=SCALE_AT + T - BURST, align_bytes=BURST)
         nc.sync.dma_start(gam_sb[:], gam)
         nc.sync.dma_start(bet_sb[:], bet)
 
         word_px = [keep.tile([P, S], U32, name="word_px%d" % o, align_bytes=64) for o in range(PASSES)]
         w_grouped = [keep.tile([P, N, PACK], BF16, name="w_grouped%d" % o, align_bytes=64) for o in range(PASSES)]
         w_codes = [keep.tile([P, N], U32, name="w_codes%d" % o, align_bytes=64) for o in range(PASSES)]
-        w_scales = [keep.tile([P, N], U8, name="w_scales%d" % o, align_bytes=64) for o in range(PASSES)]
+        w_scales = [
+            tables.tile([P, N], U8, name="w_scales%d" % o, offset=SCALE_AT + (1 + o) * BURST, align_bytes=BURST)
+            for o in range(PASSES)
+        ]
 
         for o in range(PASSES):
             nc.scalar.copy(
                 w_grouped[o][:].rearrange("p (c i) j -> p c j i", i=LINE),
-                w_raw[o][:].rearrange("p j (c i) -> p c j i", i=LINE),
+                w_raw[:, o, :].rearrange("p (j c i) -> p c j i", j=PACK, i=LINE),
             )
             nc.vector.quantize_mx(
                 out=w_codes[o][:].bitcast(FP8X4),

@@ -140,11 +140,9 @@ def tile_picked_yspade_silu_p_kernel(tc, x_words, x_scales, w1, gam, bet, offs, 
             nc.vector.scalar_tensor_tensor(
                 scaled[:, cols], y[h][:], mean_var[:, 0:1], gam_px[:, cols], ALU.subtract, ALU.mult
             )
-        stores = {QUARTER: quarters[0], 2 * QUARTER: quarters[1], S: slice(2 * QUARTER, S)}
         for cols in quarters:
             nc.vector.scalar_tensor_tensor(
                 shifted[:, cols], scaled[:, cols], rstd[:], bet_px[:, cols], ALU.mult, ALU.add
             )
             nc.scalar.activation(result[:, cols], shifted[:, cols], ACT.Silu)
-            if cols.stop in stores:
-                nc.sync.dma_start(out[:, stores[cols.stop]], result[:, stores[cols.stop]])
+            nc.sync.dma_start(out[:, cols], result[:, cols])

@@ -41,10 +41,10 @@ def tile_picked_yspade_silu_p_kernel(tc, x_words, x_scales, w1, gam, bet, offs, 
         tables = ctx.enter_context(tc.tile_pool(name="tables", bufs=1))
         psum = ctx.enter_context(tc.psum_pool(name="psum", bufs=1))
 
-        offs_sb = keep.tile([P, S // LIST_ROWS], U16, name="offs_sb")
-        lab_sb = keep.tile([P, S // LIST_ROWS], U16, name="lab_sb")
+        offs_sb = keep.tile([P, S // LIST_ROWS], U16, name="offs_sb", align_bytes=BURST)
+        lab_sb = keep.tile([P, S // LIST_ROWS], U16, name="lab_sb", align_bytes=BURST)
         scale_sb = tables.tile([P, T], U8, name="scale_sb", offset=SCALE_AT, align_bytes=BURST)
-        scale_px = keep.tile([P, PASSES * S], U8, name="scale_px", align_bytes=64)
+        scale_px = keep.tile([P, PASSES * S], U8, name="scale_px", align_bytes=BURST)
         word_sb = [keep.tile([P, T], U32, name="word_sb%d" % o, align_bytes=BURST) for o in range(PASSES)]
         w_raw = keep.tile([P, PASSES, PACK * N], F32, name="w_raw", align_bytes=BURST)
         minus_half = keep.tile([P, 1], F32, name="minus_half")
@@ -68,7 +68,7 @@ def tile_picked_yspade_silu_p_kernel(tc, x_words, x_scales, w1, gam, bet, offs, 
             nc.sync.dma_start(word_sb[o][:].bitcast(I32), x_words[o].rearrange("p c j -> p (c j)").bitcast(I32))
         nc.sync.dma_start(lab_sb[:], lab)
 
-        scale_picked = keep.tile([P, S], U8, name="scale_picked", align_bytes=64)
+        scale_picked = keep.tile([P, S], U8, name="scale_picked", align_bytes=BURST)
         nc.vector.tensor_copy(scale_picked[:], scale_sb[:].indirect(offs_sb[:]))
         for base in range(0, P, QUADRANT):
             nc.sync.dma_start(
@@ -140,9 +140,12 @@ def tile_picked_yspade_silu_p_kernel(tc, x_words, x_scales, w1, gam, bet, offs, 
             nc.vector.scalar_tensor_tensor(
                 scaled[:, cols], y[h][:], mean_var[:, 0:1], gam_px[:, cols], ALU.subtract, ALU.mult
             )
-        for cols in quarters:
+        pieces = [slice(0, QUARTER // 2), slice(QUARTER // 2, QUARTER)] + quarters[1:]
+        stores = {cols.stop: cols for cols in pieces[:3] + [slice(2 * QUARTER, S)]}
+        for cols in pieces:
             nc.vector.scalar_tensor_tensor(
                 shifted[:, cols], scaled[:, cols], rstd[:], bet_px[:, cols], ALU.mult, ALU.add
             )
             nc.scalar.activation(result[:, cols], shifted[:, cols], ACT.Silu)
-            nc.sync.dma_start(out[:, cols], result[:, cols])
+            if cols.stop in stores:
+                nc.sync.dma_start(out[:, stores[cols.stop]], result[:, stores[cols.stop]])

@@ -35,7 +35,7 @@ QUARTER = S // 4
 def tile_picked_yspade_silu_p_kernel(tc, x_words, x_scales, w1, gam, bet, offs, lab, out):
     nc = tc.nc
     quarters = [slice(first, first + QUARTER) for first in range(0, S, QUARTER)]
-    banks = [slice(0, 2 * QUARTER), quarters[2], quarters[3]]
+    banks = [slice(QUARTER, 3 * QUARTER), quarters[0], quarters[3]]
     with ExitStack() as ctx:
         keep = ctx.enter_context(tc.tile_pool(name="keep", bufs=1))
         tables = ctx.enter_context(tc.tile_pool(name="tables", bufs=1))
@@ -109,8 +109,12 @@ def tile_picked_yspade_silu_p_kernel(tc, x_words, x_scales, w1, gam, bet, offs, 
 
         gam_px = keep.tile([P, S], F32, name="gam_px")
         bet_px = keep.tile([P, S], F32, name="bet_px")
-        for picked, table in ((gam_px, gam_sb), (bet_px, bet_sb)):
-            for cols in quarters:
+        eighths = [slice(0, QUARTER // 2), slice(QUARTER // 2, QUARTER)]
+        for picked, table, order in (
+            (gam_px, gam_sb, [quarters[0], quarters[1], quarters[3], quarters[2]]),
+            (bet_px, bet_sb, [quarters[1], eighths[1], quarters[3], quarters[2]]),
+        ):
+            for cols in order:
                 nc.scalar.activation(picked[:, cols], table[:].indirect(entries(lab_sb, cols)), ACT.Copy)
 
         y = [psum.tile([P, cols.stop - cols.start], F32, name="y%d" % h) for h, cols in enumerate(banks)]
@@ -131,20 +135,27 @@ def tile_picked_yspade_silu_p_kernel(tc, x_words, x_scales, w1, gam, bet, offs, 
         for h in range(len(banks)):
             nc.vector.bn_stats(stats[:, TRIPLE + h * STATS : TRIPLE + (h + 1) * STATS], y[h][:])
         nc.vector.bn_aggr(mean_var[:], stats[:])
+        nc.vector.tensor_copy(bet_px[:, eighths[0]], bet_sb[:].indirect(entries(lab_sb, eighths[0])))
         nc.gpsimd.tensor_tensor(rstd[:], mean_var[:, 1:2], minus_half[:], ALU.pow)
 
-        scaled = keep.tile([P, S], F32, name="scaled")
+        scaled = keep.tile([P, S - QUARTER], F32, name="scaled")
         shifted = keep.tile([P, S], F32, name="shifted")
         result = keep.tile([P, S], F32, name="result", align_bytes=BURST)
-        for h, cols in enumerate(banks):
+
+        def centred(cols):
+            if cols.start < S - QUARTER:
+                return scaled[:, cols]
+            return gam_px[:, cols.start - (S - QUARTER) : cols.stop - (S - QUARTER)]
+
+        for h, cols in sorted(enumerate(banks), key=lambda bank: bank[1].start):
             nc.vector.scalar_tensor_tensor(
-                scaled[:, cols], y[h][:], mean_var[:, 0:1], gam_px[:, cols], ALU.subtract, ALU.mult
+                centred(cols), y[h][:], mean_var[:, 0:1], gam_px[:, cols], ALU.subtract, ALU.mult
             )
-        pieces = [slice(0, QUARTER // 2), slice(QUARTER // 2, QUARTER)] + quarters[1:]
+        pieces = eighths + quarters[1:]
         stores = {cols.stop: cols for cols in pieces[:3] + [slice(2 * QUARTER, S)]}
         for cols in pieces:
             nc.vector.scalar_tensor_tensor(
-                shifted[:, cols], scaled[:, cols], rstd[:], bet_px[:, cols], ALU.mult, ALU.add
+                shifted[:, cols], centred(cols), rstd[:], bet_px[:, cols], ALU.mult, ALU.add
             )
             nc.scalar.activation(result[:, cols], shifted[:, cols], ACT.Silu)
             if cols.stop in stores:

from contextlib import ExitStack

import concourse.mybir as mybir

K, T, S, N, R = 1024, 2048, 512, 128, 256
FLOPS = 2 * K * N * S
EPS = 1e-4

F32 = mybir.dt.float32
BF16 = mybir.dt.bfloat16
I32 = mybir.dt.int32
U32 = mybir.dt.uint32
U16 = mybir.dt.uint16
U8 = mybir.dt.uint8
FP8X4 = mybir.dt.float8_e4m3fn_x4
ALU = mybir.AluOpType
ACT = mybir.ActivationFunctionType

P = 128
PACK = 4
PASSES = K // (P * PACK)
LINE = 4
BURST = 256
LIST_ROWS = 16
QUADRANT = 32
SCALE_ROWS = 4
SPREAD = QUADRANT // (PASSES * SCALE_ROWS)
TRIPLE = 3
STATS = 2 * TRIPLE
NO_WEIGHT = 2.0**-60
SCALE_AT = 4 * R - BURST
QUARTER = S // 4


def tile_picked_yspade_silu_p_kernel(tc, x_words, x_scales, w1, gam, bet, offs, lab, out):
    nc = tc.nc
    quarters = [slice(first, first + QUARTER) for first in range(0, S, QUARTER)]
    banks = [slice(QUARTER, 3 * QUARTER), quarters[0], quarters[3]]
    with ExitStack() as ctx:
        keep = ctx.enter_context(tc.tile_pool(name="keep", bufs=1))
        tables = ctx.enter_context(tc.tile_pool(name="tables", bufs=1))
        psum = ctx.enter_context(tc.psum_pool(name="psum", bufs=1))

        offs_sb = keep.tile([P, S // LIST_ROWS], U16, name="offs_sb", align_bytes=BURST)
        lab_sb = keep.tile([P, S // LIST_ROWS], U16, name="lab_sb", align_bytes=BURST)
        scale_sb = tables.tile([P, T], U8, name="scale_sb", offset=SCALE_AT, align_bytes=BURST)
        scale_px = keep.tile([P, PASSES * S], U8, name="scale_px", align_bytes=BURST)
        word_sb = [keep.tile([P, T], U32, name="word_sb%d" % o, align_bytes=BURST) for o in range(PASSES)]
        w_raw = keep.tile([P, PASSES, PACK * N], F32, name="w_raw", align_bytes=BURST)
        minus_half = keep.tile([P, 1], F32, name="minus_half")
        stats = keep.tile([P, TRIPLE + len(banks) * STATS], F32, name="stats")

        nc.vector.memset(scale_sb[:, : T // 2].bitcast(I32), 0)
        nc.gpsimd.memset(scale_sb[:, T // 2 :].bitcast(I32), 0)
        nc.vector.memset(scale_px[:].bitcast(I32), 0)
        nc.vector.memset(minus_half[:], -0.5)
        nc.vector.memset(stats[:, :TRIPLE], 0.0)
        nc.vector.tensor_scalar_add(stats[:, 0:1], stats[:, 0:1], NO_WEIGHT)
        nc.vector.tensor_scalar_add(stats[:, 2:3], stats[:, 2:3], S * EPS)

        unread = keep.tile([P, 1], F32, name="unread")
        nc.scalar.activation(unread[:], minus_half[:], ACT.Silu)

        nc.sync.dma_start(w_raw[:], w1.rearrange("(o p j) m -> p o (j m)", o=PASSES, j=PACK))
        nc.sync.dma_start(offs_sb[:], offs)
        nc.sync.dma_start(scale_sb[0:P:SPREAD, :].bitcast(I32), x_scales.bitcast(I32).rearrange("o i c -> i o c"))
        for o in range(PASSES):
            nc.sync.dma_start(word_sb[o][:].bitcast(I32), x_words[o].rearrange("p c j -> p (c j)").bitcast(I32))
        nc.sync.dma_start(lab_sb[:], lab)

        scale_picked = keep.tile([P, S], U8, name="scale_picked", align_bytes=BURST)
        nc.vector.tensor_copy(scale_picked[:], scale_sb[:].indirect(offs_sb[:]))
        for base in range(0, P, QUADRANT):
            nc.sync.dma_start(
                scale_px[base : base + SCALE_ROWS, :].bitcast(I32),
                scale_picked[base : base + QUADRANT : SPREAD, :].bitcast(I32),
            )

        gam_sb = tables.tile([P, R], F32, name="gam_sb", offset=SCALE_AT + BURST - 4 * R, align_bytes=BURST)
        bet_sb = tables.tile([P, R], F32, name="bet_sb", offset=SCALE_AT + T - BURST, align_bytes=BURST)
        nc.sync.dma_start(gam_sb[:], gam)
        nc.sync.dma_start(bet_sb[:], bet)

        word_px = [keep.tile([P, S], U32, name="word_px%d" % o, align_bytes=64) for o in range(PASSES)]
        w_grouped = [keep.tile([P, N, PACK], BF16, name="w_grouped%d" % o, align_bytes=64) for o in range(PASSES)]
        w_codes = [keep.tile([P, N], U32, name="w_codes%d" % o, align_bytes=64) for o in range(PASSES)]
        w_scales = [
            tables.tile([P, N], U8, name="w_scales%d" % o, offset=SCALE_AT + (1 + o) * BURST, align_bytes=BURST)
            for o in range(PASSES)
        ]

        for o in range(PASSES):
            nc.scalar.copy(
                w_grouped[o][:].rearrange("p (c i) j -> p c j i", i=LINE),
                w_raw[:, o, :].rearrange("p (j c i) -> p c j i", j=PACK, i=LINE),
            )
            nc.vector.quantize_mx(
                out=w_codes[o][:].bitcast(FP8X4),
                scales=w_scales[o][:],
                in_=w_grouped[o][:].rearrange("p m j -> p (m j)"),
            )

        def entries(table, cols):
            return table[:, cols.start // LIST_ROWS : cols.stop // LIST_ROWS]

        nc.vector.tensor_copy(word_px[0][:], word_sb[0][:].indirect(offs_sb[:]))
        for cols in banks:
            nc.vector.tensor_copy(word_px[1][:, cols], word_sb[1][:].indirect(entries(offs_sb, cols)))

        gam_px = keep.tile([P, S], F32, name="gam_px")
        bet_px = keep.tile([P, S], F32, name="bet_px")
        eighths = [slice(0, QUARTER // 2), slice(QUARTER // 2, QUARTER)]
        for picked, table, order in (
            (gam_px, gam_sb, [quarters[0], quarters[1], quarters[3], quarters[2]]),
            (bet_px, bet_sb, [quarters[1], eighths[1], quarters[3], quarters[2]]),
        ):
            for cols in order:
                nc.scalar.activation(picked[:, cols], table[:].indirect(entries(lab_sb, cols)), ACT.Copy)

        y = [psum.tile([P, cols.stop - cols.start], F32, name="y%d" % h) for h, cols in enumerate(banks)]
        for o in range(PASSES):
            for h, cols in enumerate(banks):
                nc.tensor.matmul_mx(
                    out=y[h][:],
                    lhsT=w_codes[o][:].bitcast(FP8X4),
                    lhsT_scale=w_scales[o][:],
                    rhs=word_px[o][:, cols].bitcast(FP8X4),
                    rhs_scale=scale_px[:, o * S + cols.start : o * S + cols.stop],
                    start=(o == 0),
                    stop=(o == PASSES - 1),
                )

        mean_var = keep.tile([P, 2], F32, name="mean_var")
        rstd = keep.tile([P, 1], F32, name="rstd")
        for h in range(len(banks)):
            nc.vector.bn_stats(stats[:, TRIPLE + h * STATS : TRIPLE + (h + 1) * STATS], y[h][:])
        nc.vector.bn_aggr(mean_var[:], stats[:])
        nc.vector.tensor_copy(bet_px[:, eighths[0]], bet_sb[:].indirect(entries(lab_sb, eighths[0])))
        nc.gpsimd.tensor_tensor(rstd[:], mean_var[:, 1:2], minus_half[:], ALU.pow)

        scaled = keep.tile([P, S - QUARTER], F32, name="scaled")
        shifted = keep.tile([P, S], F32, name="shifted")
        result = keep.tile([P, S], F32, name="result", align_bytes=BURST)

        def centred(cols):
            if cols.start < S - QUARTER:
                return scaled[:, cols]
            return gam_px[:, cols.start - (S - QUARTER) : cols.stop - (S - QUARTER)]

        for h, cols in sorted(enumerate(banks), key=lambda bank: bank[1].start):
            nc.vector.scalar_tensor_tensor(
                centred(cols), y[h][:], mean_var[:, 0:1], gam_px[:, cols], ALU.subtract, ALU.mult
            )
        pieces = eighths + quarters[1:]
        stores = {cols.stop: cols for cols in pieces[:3] + [slice(2 * QUARTER, S)]}
        for cols in pieces:
            nc.vector.scalar_tensor_tensor(
                shifted[:, cols], centred(cols), rstd[:], bet_px[:, cols], ALU.mult, ALU.add
            )
            nc.scalar.activation(result[:, cols], shifted[:, cols], ACT.Silu)
            if cols.stop in stores:
                nc.sync.dma_start(out[:, stores[cols.stop]], result[:, stores[cols.stop]])
